import numpy as np, ml_dtypes
CORES = [23,119,17,113]
N = 4
BF = ml_dtypes.bfloat16
def gentries(a):
    return np.ascontiguousarray(a.reshape(8, 16, -1).transpose(0, 2, 1)).reshape(8, -1)
def gtable(e):
    e = np.asarray(e); return np.ascontiguousarray(e.reshape(8, -1, 16).transpose(0, 2, 1)).reshape(128, -1).astype(np.int32)
P, M, W, CAP, S, RO = 5120, 2048, 7168, 1024, 1, 4
def parts(rng):
    x = rng.integers(0, 16, (N, 8, 16, W), dtype=np.int16)
    src = rng.integers(0, W, (N, 8, M)); trig = rng.integers(0, W, (N, 8, M))
    tg = np.ascontiguousarray(np.argsort(rng.random((N, 8, W)), axis=-1)[..., :M])
    th = rng.choice(np.array([66, 74, 80, 86, 92]), (N, 8, 1)); th[0, 0] = 66; th[1, 1] = 92
    return x, src, trig, tg, th
def dist(x, trig):
    return np.add.reduce(np.abs(np.take_along_axis(x, trig[:, :, None, :], 3) - x[..., P:]), axis=2)
def aim(rng, x, th, want):
    none = np.zeros((N, 8, M), np.int64)
    t = np.where(want, P + np.arange(M), np.where(dist(x, none) >= dist(x, none + 1), 0, 1))
    for k in range(4):
        c = rng.integers(0, W, (N, 8, M)); t = np.where((dist(x, c) < th) == want, c, t)
    return t
def aimed(rng, e, b):
    o = rng.permutation(W); t = o[~np.isin(o, b)][:M]; t[e] = b
    return t
def apart(rng, n):
    return np.stack([2 * rng.permutation(M // 2)[:n] + rng.integers(0, 2, n) for r in range(N)])
def pack(x, src, trig, tg, th):
    return {"x": x.reshape(N, 128, W).astype(np.float32).astype(BF), "src": np.stack([gtable(a) for a in src]), "trig": np.stack([gtable(a) for a in trig]),
            "tg": np.stack([gtable(a) for a in tg]), "th": np.ascontiguousarray(np.repeat(th, 16, axis=2).reshape(N, 128, 1)).astype(np.int32)}
def setup_inputs(rng):
    return pack(*parts(rng))
def setup_inputs_room(rng):
    x, src, trig, tg, th = parts(rng); x[..., 0] = 0; x[..., 1] = 15
    n = rng.choice(np.array([0, 1, CAP - 1, CAP, CAP + 1, M]), (N, 8)); n[0] = np.array([CAP, CAP + 1, M, CAP - 1, 1, 0, CAP, CAP + 1])
    n[1] = rng.permutation(np.arange(2, 10)); n[2] = rng.permutation(np.arange(10, 18))
    key = rng.random((N, 8, M)); key[0, :, M - 1] = -1.0
    want = np.argsort(np.argsort(key, axis=-1), axis=-1) < n[:, :, None]
    return pack(x, src, aim(rng, x, th, want), tg, th)
def setup_inputs_ties(rng):
    x, src, trig, tg, th = parts(rng)
    lo = rng.choice(np.array([0, 4, 7]), (N, 8, 1, 1)); lo[0, :3] = np.array([0, 4, 7]).reshape(3, 1, 1); lo[1:, 3] = 0; lo[:, 4] = 7
    x = lo + (15 - 2 * lo) * rng.integers(0, 2, (N, 8, 16, W))
    th = 8 * (15 - 2 * lo[..., 0]) + rng.integers(0, 2, (N, 8, 1)); th[0, 3] = 0; th[1, 3] = 241; th[2, 3] = 240; th[3:, 3] = rng.integers(161, 241, (N - 3, 1))
    x[1:, 3, :, 0] = 0; x[1:, 3, :, P:P + 8] = 15; trig[1:, 3, :8] = 0
    th[:, 4] = 1 + (np.arange(N)[:, None] + rng.integers(0, 7)) % 7
    m = x[:, 4, :, P:P + 8]; x[:, 4, :, :8] = np.where(np.arange(16)[:, None] < np.arange(8), 15 - m, m); trig[:, 4, :8] = np.arange(8)
    return pack(x, src, trig, tg, th)
def setup_inputs_alike(rng):
    x, src, trig, tg, th = parts(rng); e = np.arange(M); h = min(P, M - M // 16); low = e % 16 < 8
    for q in range(N):
        tg[q, 0] = P + rng.permutation(M)
        tg[q, 1] = rng.permutation(np.concatenate([rng.permutation(P)[:h], P + rng.permutation(M)[:M - h]]))
        tg[q, 2] = P + (2 * rng.permutation(M // 2)[:, None] + np.array([0, 1])).reshape(-1)
        tg[q, 3, low] = P + 2 * rng.permutation(M // 2); tg[q, 3, ~low] = rng.permutation(P)[:M // 2]
        o = rng.permutation(W); tg[q, 5] = o[np.argsort((o + rng.integers(0, 16)) % 16, kind="stable")][:M]
        tg[q, 7] = e if q % 2 == 0 else W - 1 - e
    x[:, 2, :, P + 1::2] = x[:, 2, :, P::2]; trig[:, 2, 1::2] = trig[:, 2, ::2]
    src[:, 3] = rng.integers(0, P, (N, M)); trig[:, 3] = np.where(low, P + e, rng.integers(0, P, (N, M))); th[:, 3] = 1
    x[:, 4, :, P:] = rng.integers(0, 8, (N, 16, M)); x[:, 5, :, P:] = rng.integers(8, 16, (N, 16, M)); th[:, 5] = 241
    src[:, 6] = rng.choice(np.array([0, W - 1, P - 1, P]), (N, M)); trig[:, 6] = rng.choice(np.array([0, W - 1, P - 1, P]), (N, M))
    trig[:, 7] = P + e; th[:, 7] = 1
    return pack(x, src, trig, tg, th)
def setup_inputs_cold(rng):
    x, src, trig, tg, th = parts(rng); q = rng.permutation(N); g = rng.permutation(8)
    th[q[0]] = 0; th[q[1]] = 241
    th[:, g[:3]] = 0; th[3, g[1]] = 80; th[rng.integers(0, N), g[2]] = 80
    for k in g[3:6]:
        th[:, k] = 1; src[:, k] = rng.integers(0, P, (N, M)); trig[:, k] = rng.integers(0, P, (N, M))
    for k, n in ((g[3], 5), (g[4], int(rng.integers(2, 18)))):
        e = np.sort(apart(rng, n), axis=1)
        for r in range(N):
            trig[r, k, e[r]] = P + e[r]; tg[r, k] = aimed(rng, e[r], P + np.roll(e[(r + S) % N], -1))
    k = g[5]; n = int(rng.integers(2, 18)); e = apart(rng, 2 * n); a = e[:, :n]; b = e[:, n:]
    for r in range(N):
        s = (r + S) % N
        x[r, k][:, P + a[r]] = rng.integers(0, 8, (16, n)); trig[r, k, a[r]] = P + a[r]; src[r, k, b[r]] = P + b[r]
        tg[r, k] = aimed(rng, np.concatenate([a[r], b[r] ^ 1]), P + np.concatenate([b[s], a[s]]))
    return pack(x, src, trig, tg, th)
def setup_inputs_spread(rng):
    x, src, trig, tg, th = parts(rng)
    level = rng.integers(0, 16, (N, 8, 1, W)).astype(np.float32); width = np.exp2(rng.integers(-1, 4, (N, 8, 1, W))).astype(np.float32)
    x = np.clip(np.rint(level + width * rng.standard_normal((N, 8, 16, W), dtype=np.float32)), 0, 15).astype(np.int16)
    src = np.minimum((W * rng.random((N, 8, M)) ** 3).astype(np.int64), W - 1); trig = np.minimum((W * rng.random((N, 8, M)) ** 2).astype(np.int64), W - 1)
    tg[:, 1::2] = np.sort(tg[:, 1::2], axis=-1); th = rng.integers(20, 161, (N, 8, 1))
    return pack(x, src, trig, tg, th)
def check_inputs(d):
    bad = []
    v = np.asarray(d["x"], np.float32)
    if not (np.min(v) >= 0 and np.max(v) <= 15 and np.all(v == np.floor(v))): bad.append("numbers of x")
    for k, lo, hi in (("src", 0, W - 1), ("trig", 0, W - 1), ("tg", 0, W - 1), ("th", 0, 241)):
        if np.min(d[k]) < lo or np.max(d[k]) > hi: bad.append("range of " + k)
    o = np.sort(np.stack([gentries(a) for a in d["tg"]]), axis=-1)
    if np.any(o[..., 1:] == o[..., :-1]): bad.append("targets of a rank and group differ")
    t = np.asarray(d["th"]).reshape(N, 8, 16)
    if np.any(t != t[:, :, :1]): bad.append("rows of th alike in a group")
    return bad
def reference(x, src, trig, tg, th):
    v = x.astype(np.float32).astype(np.int32).reshape(N, 8, 16, W); lim = th.astype(np.int64).reshape(N, 8, 16)[:, :, :1]
    so = np.stack([gentries(a) for a in src]).astype(np.int64); tr = np.stack([gentries(a) for a in trig]).astype(np.int64); ta = np.stack([gentries(a) for a in tg]).astype(np.int64)
    mate = np.arange(M) ^ 1
    for rnd in range(RO):
        m = v[..., P:]
        far = np.add.reduce(np.abs(np.take_along_axis(v, tr[:, :, None, :], 3) - m), axis=2)
        c = (far < lim).astype(np.int64); go = (c == 1) & (np.add.accumulate(c, axis=2) <= CAP)
        a = np.where(m >= 8, 15 - np.take_along_axis(v, so[:, :, None, :], 3), -1)
        nv = v + 0; ns = so + 0; nt = tr + 0; ng = ta + 0
        for q in range(N):
            r = (q + S) % N
            for g in range(8):
                i = np.flatnonzero(go[q, g]); b = ta[q, g, i]; col = a[q, g][:, i]
                nv[r, g][:, b] = np.where(col >= 0, col, v[r, g][:, b])
                j = b >= P; e = b[j] - P
                nt[r, g, e] = so[r, g, e]; ns[r, g, e] = so[q, g, i[j]]
                hit = np.zeros(M, bool); hit[e] = True
                ng[r, g] = np.where(hit != hit[mate], ta[r, g][mate], ta[r, g])
        v, so, tr, ta = nv, ns, nt, ng
    return {"yx": v.reshape(N, 128, W).astype(np.float32).astype(BF), "ysrc": np.stack([gtable(a) for a in so]).astype(np.float32),
            "ytrig": np.stack([gtable(a) for a in tr]).astype(np.float32), "ytg": np.stack([gtable(a) for a in ta]).astype(np.float32)}

@@ -1,0 +1,534 @@
+from concourse.mybir import AluOpType, ActivationFunctionType
+
+ALU = AluOpType
+ACT = ActivationFunctionType
+P, M, W, CAP, RO = 5120, 2048, 7168, 1024, 4
+PAD = 128
+YC = PAD + W
+ZW = YC + M
+K = 16384.0
+CH = 512
+CFG = {
+    "x": [0, 1792, 3840, 5888, 7168],
+    "d": [0, 256, 640, 1024, 1664, 2048],
+    "dgv": 512,
+    "g10": "vvva", "y0": "vvva",
+    "g1": 640, "g2": 640, "g1l": 512, "g2l": 512, "g20": 0,
+}
+
+SCRATCH = {
+    "Z": ("sbuf", [128, ZW], "bfloat16"), "LT": ("sbuf", [128, ZW], "bfloat16"),
+    "LO": ("sbuf", [128, RO * M], "bfloat16"), "LAND": ("sbuf", [128, RO * M], "bfloat16"),
+    "MB": ("sbuf", [128, M], "bfloat16"), "DB": ("sbuf", [128, M], "bfloat16"), "AB": ("sbuf", [128, M], "bfloat16"),
+    "GB": ("sbuf", [128, M], "bfloat16"), "IW": ("sbuf", [128, 16 + M], "bfloat16"), "I2": ("sbuf", [128, M], "bfloat16"),
+    "DG": ("sbuf", [128, M], "bfloat16"), "OUT": ("sbuf", [128, W], "bfloat16"),
+    "LI": ("sbuf", [128, 384], "int32"), "THI": ("sbuf", [128, 8], "int32"),
+    "TAO": ("sbuf", [128, 128], "uint16"), "TAU": ("sbuf", [128, 128], "uint16"),
+    "S0U": ("sbuf", [128, 128], "uint16"), "TLU": ("sbuf", [128, 128], "uint16"), "SLU": ("sbuf", [128, 128], "uint16"),
+    "SSO": ("sbuf", [128, RO * 128], "uint16"), "SSI": ("sbuf", [128, RO * 128], "uint16"),
+    "LOC": ("sbuf", [128, 448], "uint16"), "INV": ("sbuf", [128, 128], "uint16"), "IDX": ("sbuf", [128, 128], "uint16"),
+    "SA": ("sbuf", [128, 256], "float32"), "SB": ("sbuf", [128, 256], "float32"),
+    "TA": ("sbuf", [128, 128], "float32"), "DD": ("sbuf", [128, 128], "float32"), "TR": ("sbuf", [128, 256], "float32"),
+    "U0": ("sbuf", [128, 256], "float32"), "U1": ("sbuf", [128, 256], "float32"), "SLOT": ("sbuf", [128, 256], "float32"),
+    "TM": ("sbuf", [128, 256], "float32"), "THR": ("sbuf", [128, 256], "float32"), "FIN": ("sbuf", [128, 384], "float32"),
+    "NHB": ("sbuf", [128, 128], "bfloat16"), "XP": ("sbuf", [128, 128], "bfloat16"), "FL": ("sbuf", [128, 128], "bfloat16"),
+    "C0": ("sbuf", [128, 128], "bfloat16"), "C1": ("sbuf", [128, 128], "bfloat16"), "SC": ("sbuf", [128, 128], "bfloat16"),
+    "RI": ("sbuf", [128, 16], "int32"), "RJ": ("sbuf", [128, 16], "int32"), "RK": ("sbuf", [128, 8], "int32"),
+    "RL": ("sbuf", [128, 16], "float32"), "CL": ("sbuf", [128, 16], "float32"), "HM": ("sbuf", [128, 64], "float32"),
+    "RAMP": ("sbuf", [128, 128], "float32"), "KR": ("sbuf", [128, 128], "bfloat16"),
+    "ONE": ("sbuf", [128, 144], "float32"), "W32": ("sbuf", [128, 6 * 128], "float32"), "BG": ("sbuf", [128, 144], "float32"),
+    "WB": ("sbuf", [128, 9 * 128], "bfloat16"), "BB": ("sbuf", [128, 4 * 144], "bfloat16"),
+}
+for _b in range(8):
+    SCRATCH["PS%d" % _b] = ("psum", [128, 512], "float32")
+
+NDMA = 20
+SEMAPHORES = (["qv", "qa", "qp", "qg", "sent", "ata"] + ["d%d" % i for i in range(NDMA)]
+              + ["as%d" % t for t in range(RO)] + ["al%d_%d" % (t, c) for t in range(RO) for c in range(4)])
+
+
+def rank_program(g, core, T, topo):
+    rank = T.rank_of(core)
+    if rank is None:
+        return
+    dst = T.cores[(rank + 1) % len(T.cores)]
+    rid, pid, _ = topo.addr(dst)
+    emask = topo.mask(core, dst)
+    neng = len(topo.engines(core, dst))
+    src_core = T.cores[(rank - 1) % len(T.cores)]
+    nin = len(topo.engines(src_core, core))
+    odd = rank % 2
+
+    Q = {"v": g.vector, "a": g.scalar, "p": g.tensor, "g": g, "s": g.sync}
+    count = {"qv": 0, "qa": 0, "qp": 0, "qg": 0}
+    known = {q: {} for q in Q}
+    hist = {}
+    clock = {}
+    ndma = [0]
+    sent = [0]
+    stores = []
+
+    def ap(name, a=0, b=None, step=1):
+        t = T[name]
+        if b is None:
+            b = t.shape[1]
+        return (name, a, b, t[:, a:b] if step == 1 else t[:, a:b:step])
+
+    def col(name, j):
+        return ap(name, j, j + 1)
+
+    def wait(q, tok):
+        if known[q].get(tok[0], 0) >= tok[1]:
+            return
+        Q[q].wait_ge(T.sem[tok[0]], tok[1])
+        for s, v in clock.get(tok, {tok[0]: tok[1]}).items():
+            if known[q].get(s, 0) < v:
+                known[q][s] = v
+
+    def order(q, reads, writes, ext):
+        need = {}
+        for regs, w in ((reads, False), (writes, True)):
+            for (name, a, b, _) in regs:
+                ps = name.startswith("PS")
+                for (a2, b2, w2, q2, tok) in hist.get(name, []):
+                    if ps:
+                        hit = q2 != q or (q != "p" and (w or w2) and a < b2 and a2 < b)
+                    else:
+                        hit = (w or w2) and a < b2 and a2 < b
+                    if hit and need.get(tok[0], 0) < tok[1]:
+                        need[tok[0]] = tok[1]
+        for tok in list(ext) + sorted(need.items()):
+            wait(q, tuple(tok))
+
+    def note(q, reads, writes, tok):
+        c = dict(known[q])
+        c[tok[0]] = tok[1]
+        clock[tok] = c
+        for regs, w in ((reads, False), (writes, True)):
+            for (name, a, b, _) in regs:
+                h = hist.setdefault(name, [])
+                if w:
+                    h[:] = [e for e in h if not (a <= e[0] and e[1] <= b)]
+                h.append((a, b, w, q, tok))
+
+    def run(q, reads, writes, fn, ext=()):
+        order(q, reads, writes, ext)
+        s = "q" + q
+        count[s] += 1
+        fn().then_inc(T.sem[s], 1)
+        note(q, reads, writes, (s, count[s]))
+
+    def dma(q, out, in_, reads, writes):
+        order(q, reads, writes, ())
+        s = "d%d" % ndma[0]
+        ndma[0] += 1
+        Q[q].dma_start(out, in_).then_inc(T.sem[s], 16)
+        note(q, reads, writes, (s, 16))
+        return (s, 16)
+
+    def send(land, src, sem):
+        order("g", [src], [], ())
+        g.remote_dma(land[3], src[3], T.sem[sem], T.sem.sent, pid, rid, emask)
+        sent[0] += neng
+
+    def aps(*xs):
+        return [x for x in xs if isinstance(x, tuple)]
+
+    def raw(x):
+        return x[3] if isinstance(x, tuple) else x
+
+    def ind(win, off):
+        return win[3].indirect(off[3])
+
+    def ts(out, in0, s1, s2, op0, op1=None, off=None, ext=()):
+        i0 = in0[3] if off is None else ind(in0, off)
+        if op1 is None:
+            run("v", aps(in0, s1, off), [out], lambda: g.vector.tensor_scalar(out[3], i0, raw(s1), None, op0), ext)
+        else:
+            run("v", aps(in0, s1, s2, off), [out], lambda: g.vector.tensor_scalar(out[3], i0, raw(s1), raw(s2), op0, op1), ext)
+
+    def tt(out, in0, in1, op, off=None, ext=()):
+        i0 = in0[3] if off is None else ind(in0, off)
+        run("v", aps(in0, in1, off), [out], lambda: g.vector.tensor_tensor(out[3], i0, in1[3], op), ext)
+
+    def cp(out, in_, off=None, ext=()):
+        i0 = in_[3] if off is None else ind(in_, off)
+        run("v", aps(in_, off), [out], lambda: g.vector.tensor_copy(out[3], i0), ext)
+
+    def act(out, in_, func=ACT.Identity, bias=0.0, scale=1.0, off=None, ext=()):
+        i0 = in_[3] if off is None else ind(in_, off)
+        run("a", aps(in_, bias, scale, off), [out],
+            lambda: g.scalar.activation(out[3], i0, func, bias=raw(bias), scale=raw(scale)), ext)
+
+    def gather(q, out, win, off, ext=()):
+        if q == "v":
+            cp(out, win, off, ext)
+        else:
+            act(out, win, off=off, ext=ext)
+
+    def mm(out, pairs, start=True, stop=True, ext=()):
+        def fn():
+            for i, (l, r) in enumerate(pairs):
+                ins = g.tensor.matmul(out[3], l[3], r[3], start and i == 0, stop and i == len(pairs) - 1)
+            return ins
+        run("p", [x for pr in pairs for x in pr], [out], fn, ext)
+
+    def iota(out, pattern, base, cm, flt=True):
+        if flt:
+            run("g", [], [out], lambda: g.iota(out[3], pattern, base, cm, allow_small_or_imprecise_dtypes=True))
+        else:
+            run("g", [], [out], lambda: g.iota(out[3], pattern, base, cm))
+
+    def sel(out, in_, pattern, cmp, fill, base, cm):
+        run("g", [in_], [out], lambda: g.affine_select(out[3], in_[3], pattern, cmp, fill, base, cm))
+
+    def chunk(name, c, base=0, n=CH):
+        return ap(name, base + c * n, base + (c + 1) * n)
+
+    def lst(name, c, base=0, n=CH):
+        return ap(name, base + c * n // 16, base + (c + 1) * n // 16)
+
+    def span(name, a, b, base=0):
+        return ap(name, base + a, base + b)
+
+    def lspan(name, a, b, base=0):
+        return ap(name, base + a // 16, base + b // 16)
+
+    BF, BH, BL, BS = 0, 1, 2, 3
+
+    def wrap(out, kind, name, a, b, start=True, stop=True):
+        mm(out, [(ap("BB", kind * 144 + 15 - r, kind * 144 + 143 - r), ap(name, a + r, b, 16)) for r in range(16)], start, stop)
+
+    def band(kind, scale):
+        act(ap("BB", kind * 144, kind * 144 + 144), ap("BG"), scale=scale)
+
+    I32, PM32, SWI, B32, W032, W132 = [ap("W32", i * 128, (i + 1) * 128) for i in range(6)]
+    IB, N16, DSG, PMB, NBK, W0, W1, KI, NKI = [ap("WB", i * 128, (i + 1) * 128) for i in range(9)]
+    HC, LC, M01, M23, WS, WL, H57, IC, SG, IN7, TH, NTH = [col("CL", j) for j in range(12)]
+    R4 = col("RL", 4)
+    ZX, ZA, LTX = ap("Z", 0, YC), ap("Z"), ap("LT", 0, YC)
+    XB, DBN = CFG["x"], CFG["d"]
+
+    TG, SRC, TRG = ap("LI", 0, 128), ap("LI", 128, 256), ap("LI", 256, 384)
+    dma("s", TG[3], T.tg[:], [], [TG])
+    for c in range(len(XB) - 1):
+        z = span("Z", XB[c], XB[c + 1], PAD)
+        dma("s", z[3], T.x[:, XB[c]:XB[c + 1]], [], [z])
+    dma("a", SRC[3], T.src[:], [], [SRC])
+    dma("a", TRG[3], T.trig[:], [], [TRG])
+    dma("a", col("THI", 0)[3], T.th[:], [], [col("THI", 0)])
+
+    iota(ap("RI"), [[-1, 16]], 16, 1, False)
+    iota(ap("RAMP"), [[1, 128]], 0, 0)
+    iota(ap("ONE"), [[0, 144]], 1, 0)
+    one = ap("ONE", 0, 128)
+    sel(ap("BG"), ap("ONE"), [[0, 9], [1, 16]], ALU.is_equal, 0.0, -15, 0)
+    sel(I32, one, [[-1, 128]], ALU.is_equal, 0.0, 0, 1)
+    run("v", [], [ap("Z", 0, PAD)], lambda: g.vector.memset(T.Z[:, 0:PAD], 0.0))
+    ts(ap("RJ"), ap("RI"), 15, None, ALU.bitwise_and)
+    run("v", [], [ap("C1")], lambda: g.vector.memset(T.C1[:], 0.0))
+    ts(ap("RL"), ap("RJ"), 0.0, None, ALU.is_equal)
+    tt(ap("CL", 0, 2), ap("RL", 0, 2), ap("RL", 2, 4), ALU.add)
+    tt(ap("CL", 2, 4), ap("RL", 0, 4, 2), ap("RL", 1, 4, 2), ALU.add)
+    ts(ap("LT", 0, 128), ap("RAMP"), LC, None, ALU.mult)
+    ts(ap("HM"), ap("RAMP", 0, 64), HC, None, ALU.mult)
+    ts(H57, col("RL", 2), float(YC // 128), None, ALU.mult)
+    n = 128
+    while n < 2048:
+        ts(ap("LT", n, 2 * n), ap("LT", 0, n), col("HM", n // 128), None, ALU.add)
+        n *= 2
+    ts(ap("TAO"), TG, float(PAD), None, ALU.add)
+    send(ap("TAU"), ap("TAO"), "ata")
+    ATA = [("ata", nin)]
+    act(ap("LT", YC, ZW), ap("LT", 0, M), bias=H57, scale=M23)
+    ts(ap("LT", 2048, 4096), ap("LT", 0, 2048), col("HM", 16), None, ALU.add)
+    ts(ap("LT", 4096, YC), ap("LT", 0, YC - 4096), col("HM", 32), None, ALU.add)
+
+    sel(ap("BG"), ap("BG"), [[-16, 9], [0, 16]], ALU.is_ge, 0.0, 0, 1)
+    sel(B32, one, [[-16, 8], [0, 16]], ALU.is_ge, 0.0, 0, 1)
+    sel(ap("BG"), ap("BG"), [[16, 9], [0, 16]], ALU.is_ge, 0.0, 15, -1)
+    sel(B32, B32, [[16, 8], [0, 16]], ALU.is_ge, 0.0, 15, -1)
+    sel(PM32, one, [[-2, 64], [0, 2]], ALU.is_ge, 0.0, 0, 1)
+    sel(W032, B32, [[-1, 128]], ALU.is_ge, 0.0, 0, 1)
+    sel(W132, B32, [[-2, 64], [1, 2]], ALU.is_ge, 0.0, -1, 1)
+    sel(W032, W032, [[-1, 128]], ALU.not_equal, float(CAP + 8), 0, 1)
+    sel(PM32, PM32, [[2, 64], [0, 2]], ALU.is_ge, 0.0, 1, -1)
+    sel(W132, W132, [[-2, 64], [1, 2]], ALU.not_equal, float(CAP + 8), -1, 1)
+    iota(ap("KR"), [[-1, 128]], 0, 0)
+    sel(SWI, PM32, [[-1, 128]], ALU.not_equal, -1.0, 0, 1)
+
+    cm, cb = (-1.0, 16.0) if odd else (1.0, 1.0)
+
+    def conv(q, c):
+        z = span("Z", XB[c], XB[c + 1], PAD)
+        if q == "v":
+            ts(z, z, cm, cb, ALU.mult, ALU.add)
+        else:
+            act(z, z, bias=cb, scale=cm)
+
+    S = [ap("SA"), ap("SB")]
+
+    def sl(i):
+        return ap(S[i][0], 0, 128)
+
+    def ss(i):
+        return ap(S[i][0], 128, 256)
+
+    T1P, TL = ap("PS2", 0, 128), ap("PS2", 128, 256)
+    dv = M - CFG["dgv"]
+    conv("a", 0)
+    ts(ap("CL", 4, 6), ap("RL", 0, 4, 2), 128.0, None, ALU.mult)
+    ts(col("RK", 0), col("RJ", 0), 1, None, ALU.bitwise_and)
+    cp(IC, col("RJ", 0))
+    tt(ap("CL", 4, 6), ap("CL", 4, 6), ap("RL", 1, 4, 2), ALU.add)
+    ts(SG, col("RK", 0), -2.0, 1.0, ALU.mult, ALU.add)
+    ts(IN7, col("RL", 0), 7.0, None, ALU.mult)
+    cp(TH, col("THI", 0))
+    ts(NTH, col("THI", 0), -1.0, None, ALU.mult)
+    act(IB, I32)
+    act(span("DG", 0, dv), LTX, scale=M01, off=lspan("TAU", 0, dv), ext=ATA)
+    conv("v", 1)
+    ts(ss(0), SRC, float(PAD), None, ALU.add)
+    ts(ap("S0U"), SRC, float(PAD), None, ALU.add)
+    ts(ap("TR", 0, 128), TRG, float(PAD), None, ALU.add)
+    ts(ap("TLU"), TRG, float(PAD), None, ALU.add)
+    cp(ap("TA"), TG)
+    ts(ap("IW", 0, 16), ap("Z", 0, 16), R4, None, ALU.add)
+    conv("v", 2)
+    ts(span("DG", dv, M), LTX, M01, None, ALU.mult, off=lspan("TAU", dv, M), ext=ATA)
+    cp(col("LT", 0), R4)
+    run("v", [ap("DG"), ap("LT", YC, ZW), ap("TAU")], [LTX],
+        lambda: g.vector.tensor_tensor(ind(LTX, ap("TAU")), T.DG[:], T.LT[:, YC:ZW], ALU.add), ATA)
+    band(BF, 1.0)
+    conv("a", 3)
+
+    FAR = [ap("PS0", 0, 64), ap("PS0", 64, 128), ap("PS0", 0, 128)]
+    NH, VV, F2 = ap("PS4", 0, 128), ap("PS4", 128, 256), ap("PS4", 256, 512)
+    PAIR, IXP, SWP = ap("PS3", 0, 128), ap("PS3", 128, 256), ap("PS3", 256, 512)
+    QB = [ap("PS6"), ap("PS7"), ap("PS0"), ap("PS1")]
+    FL = ap("FL")
+    gs, gb = (-16.0, 144.0) if odd else (16.0, -128.0)
+
+    def flips(t):
+        if t == 1:
+            ts(FL, ap("XP"), 0.0, None, ALU.is_equal)
+        else:
+            tt(FL, FL, ap("XP"), ALU.is_equal)
+
+    def watch(t):
+        mm(ap("PS3", 256, 384), [(I32, ap("TR", 0, 128))] + ([(I32, ap("TR", 128, 256))] if t > 1 else []) + [(KI, ap("NHB"))])
+        mm(ap("PS3", 384, 512), [(I32, ss((t + 1) % 2)), (NKI, ap("NHB"))])
+
+    def watch2(shift):
+        act(ap("TR", 0, 128), ap("PS3", 256, 384), ACT.Relu, bias=shift - K)
+        act(ap("TR", 128, 256), ap("PS3", 384, 512), ACT.Relu, bias=shift)
+
+    def lower(t, c):
+        mm(QB[c], [(N16, chunk("LAND", c, t * M))], False, True, ext=[("al%d_%d" % (t, c), nin)])
+
+    def merge(t, c):
+        tt(chunk("Z", c, YC), chunk("LAND", c, t * M), QB[c], ALU.max, ext=[("al%d_%d" % (t, c), nin)])
+
+    def gate0(c):
+        ts(chunk("GB", c, 0, 1024), chunk("Z", c, PAD + P, 1024), 8.5, 16.0, ALU.is_lt if odd else ALU.is_gt, ALU.mult)
+
+    for t in range(RO):
+        cur, old = t % 2, (t + 1) % 2
+        last = t == RO - 1
+        win = ZX if t == 0 else ZA
+        if t == 0:
+            tb = [ap("PS6"), ap("PS7"), ap("PS5"), ap("PS3")]
+            for c in range(4):
+                act(chunk("DB", c), ZX, scale=-1.0, off=lst("TLU", c))
+                mm(tb[c], [(IB, chunk("Z", c, PAD + P)), (IB, chunk("DB", c))])
+                if c > 0:
+                    act(chunk("AB", c - 1), tb[c - 1], ACT.Abs)
+                if c == 2:
+                    wrap(FAR[0], BF, "AB", 0, 1024)
+            act(NBK, B32, scale=-K)
+            act(chunk("AB", 3), tb[3], ACT.Abs)
+            wrap(FAR[1], BF, "AB", 1024, 2048)
+            act(W0, W032, scale=K)
+            band(BL, WL)
+            gate0(0)
+            ts(ap("C0"), FAR[2], TH, None, ALU.is_lt)
+        else:
+            nd = len(DBN) - 1
+            wrap(ap("PS5", 0, 128), BL, "I2", 0, M)
+            for c in range(nd):
+                gather("a", span("MB", DBN[c], DBN[c + 1]), ZA, lspan("LOC", DBN[c], DBN[c + 1], P // 16))
+                if c == 0:
+                    act(ap("NHB"), NH)
+                    mm(PAIR, [(PMB, ap("NHB"))])
+                if c == 1:
+                    act(ap("XP"), PAIR, ACT.Abs, bias=-1.0)
+            wrap(ap("PS5", 128, 256), BS, "I2", 0, M)
+            for c in range(nd):
+                a, b = DBN[c], DBN[c + 1]
+                tt(span("DB", a, b), win, span("MB", a, b), ALU.subtract, off=lspan("TLU", a, b))
+                if c == 1:
+                    flips(t)
+                    mm(IXP, [(N16, ap("KR")), (DSG, FL)])
+                    mm(ap("PS4", 256, 384), [(IB, FL)])
+                    mm(ap("PS4", 384, 512), [(IB, FL)])
+                    act(ap("THR", 0, 128), FL, bias=TH, scale=NTH)
+                    act(ap("THR", 128, 256), FL, scale=TH)
+                if b == 1024:
+                    wrap(FAR[0], BF, "DB", 0, 1024, True, False)
+                if c == 2:
+                    ts(ap("IDX"), IXP, IC, None, ALU.add)
+                if b <= 1024:
+                    ts(span("AB", a, b), span("DB", a, b), 0.0, -2.0, ALU.min, ALU.mult)
+                else:
+                    act(span("AB", a, b), span("DB", a, b), ACT.Abs)
+                if b == 1024:
+                    wrap(FAR[0], BF, "AB", 0, 1024, False, True)
+            wrap(FAR[1], BF, "AB", 1024, 2048)
+            for c in range(4):
+                act(chunk("GB", c), ap("MB"), ACT.Relu, bias=gb, scale=gs, off=lst("IDX", c))
+            tt(ap("U0", 0, 128), sl(old), NH, ALU.mult)
+            tt(ap("U0", 128, 256), ss(old), NH, ALU.mult)
+            tt(S[cur], ap("U0"), ap("PS5", 0, 256), ALU.add)
+            tt(ap("U1"), S[cur], F2, ALU.mult)
+            mm(SWP, [(SWI, ap("U1"))])
+            tt(ap("C0"), FAR[2], ap("THR", 0, 128), ALU.is_lt)
+            tt(ap("C1"), FAR[2], ap("THR", 128, 256), ALU.is_lt)
+        mm(VV, [(W0, ap("C0"))] + ([(W1, ap("C1"))] if t > 0 else []), True, False)
+        run("v", [ap("C0"), ap("C1"), IN7], [ap("SC")],
+            lambda: g.vector.tensor_tensor_scan(T.SC[:], T.C0[:], T.C1[:], IN7[3], ALU.add, ALU.add))
+        mm(VV, [(NBK, ap("SC"))], False, True)
+        sso = ap("SSO", t * 128, (t + 1) * 128)
+        if t == 0:
+            wrap(ap("PS6", 0, 448), BL, "LT", PAD, YC)
+            tt(ap("TM", 128, 256), ss(0), VV, ALU.min)
+            cp(sso, ap("TM", 128, 256))
+            gate0(1)
+            slu = ("SSO", t * 128)
+        else:
+            tt(ap("SLOT", 128, 256), ss(cur), ap("PS3", 384, 512), ALU.add)
+            tt(ap("SLOT", 0, 128), sl(cur), ap("PS3", 256, 384), ALU.add)
+            tt(ap("TM", 128, 256), ap("SLOT", 128, 256), VV, ALU.min)
+            tt(ap("TM", 0, 128), ap("SLOT", 0, 128), VV, ALU.min)
+            cp(sso, ap("TM", 128, 256))
+            cp(ap("SLU"), ap("TM", 0, 128))
+            slu = ("SLU", 0)
+        send(ap("SSI", t * 128, (t + 1) * 128), sso, "as%d" % t)
+        for c in range(4):
+            tt(chunk("LO", c, t * M), win, chunk("GB", c), ALU.min, off=lst(slu[0], c, slu[1]))
+            send(chunk("LAND", c, t * M), chunk("LO", c, t * M), "al%d_%d" % (t, c))
+        AS = [("as%d" % t, nin)]
+        if t == 0:
+            act(ap("DG"), LTX, off=ap("S0U"))
+            wrap(ap("PS5", 0, 128), BL, "DG", 0, M)
+            act(N16, I32, scale=-16.0)
+            band(BH, R4)
+            band(BS, WS)
+            act(DSG, I32, scale=SG)
+            act(PMB, PM32)
+            act(W1, W132, scale=K)
+            act(KI, I32, scale=K)
+            act(NKI, I32, scale=-K)
+            act(ap("MB"), LTX, off=ap("TLU"))
+            act(sl(0), ap("PS5", 0, 128))
+            wrap(ap("PS5", 128, 256), BL, "MB", 0, M)
+            cp(ap("LOC"), ap("PS6", 0, 448))
+            ts(ap("INV"), ap("PS6", P // 16, 448), float(16 - YC), None, ALU.add)
+            for c in range(4):
+                gather(CFG["g10"][c], chunk("IW", c, 16), LTX, lst("SSI", c, t * 128), AS)
+            for c in range(4):
+                gather(CFG["y0"][c], chunk("Z", c, YC), ZX, lst("TAU", c))
+            tt(ap("DD"), ap("PS5", 128, 256), sl(0), ALU.subtract)
+            v = M - CFG["g20"]
+        else:
+            watch(t)
+            watch2(0.0)
+            v = M - CFG["g1l" if last else "g1"]
+            gather("a", span("IW", 0, v, 16), LTX, lspan("SSI", 0, v, t * 128), AS)
+            gather("v", span("IW", v, M, 16), LTX, lspan("SSI", v, M, t * 128), AS)
+            if not last:
+                tt(ap("DD"), TL, sl(cur), ALU.subtract)
+            v = M - CFG["g2l" if last else "g2"]
+        for q, a, b in (("a", 0, 1024), ("a", 1024, v), ("v", v, M)):
+            if a < b:
+                gather(q, span("I2", a, b), ap("IW"), lspan("INV", a, b))
+        for c in range(4):
+            mm(QB[c], [(IB, chunk("Z", c, YC))], True, False)
+        for c in range(3):
+            lower(t, c)
+            merge(t, c)
+        if last:
+            lower(t, 3)
+            merge(t, 3)
+            wrap(NH, BH, "I2", 0, M)
+            wrap(ap("PS5", 128, 256), BS, "I2", 0, M)
+        else:
+            wrap(ap("PS4", 0, 64), BH, "I2", 0, 1024)
+            lower(t, 3)
+            wrap(ap("PS4", 64, 128), BH, "I2", 1024, 2048)
+            merge(t, 3)
+            tt(T1P, ap("DD"), NH, ALU.mult)
+            tt(TL, T1P, sl(cur), ALU.add)
+            cp(ap("TLU"), TL)
+
+    om, ob = (-1.0, 16.0) if odd else (1.0, -1.0)
+    cur = (RO - 1) % 2
+
+    def outv(c):
+        ts(chunk("OUT", c), ZA, om, ob, ALU.mult, ALU.add, off=lst("LOC", c))
+
+    def outa(c):
+        act(chunk("OUT", c), ZA, bias=ob, scale=om, off=lst("LOC", c))
+
+    def store(a, b):
+        o = ap("OUT", a * CH, b * CH)
+        stores.append(dma("s", T.yx[:, a * CH:b * CH], o[3], [o], []))
+
+    def small(y, i):
+        o = ap("FIN", 128 * i, 128 * i + 128)
+        stores.append(dma("s", y[:], o[3], [o], []))
+
+    outv(0)
+    outa(7)
+    store(0, 1)
+    store(7, 8)
+    outv(1)
+    outv(2)
+    act(ap("NHB"), NH)
+    mm(PAIR, [(PMB, ap("NHB"))])
+    watch(RO)
+    outa(8)
+    act(ap("XP"), PAIR, ACT.Abs, bias=-1.0)
+    watch2(float(-PAD))
+    outa(9)
+    store(1, 3)
+    store(8, 10)
+    tt(ap("U0", 0, 128), ss(cur), NH, ALU.mult)
+    flips(RO)
+    mm(ap("PS4", 256, 384), [(IB, FL)])
+    tt(ap("FIN", 128, 256), ap("TR", 0, 128), ap("TR", 128, 256), ALU.add)
+    tt(TL, ap("U0", 0, 128), ap("PS5", 128, 256), ALU.add)
+    tt(ap("U1", 0, 128), ap("TA"), ap("PS4", 256, 384), ALU.mult)
+    mm(ap("PS3", 256, 384), [(SWI, ap("U1", 0, 128))])
+    ts(ap("FIN", 0, 128), TL, float(-PAD), None, ALU.add)
+    outv(3)
+    tt(ap("FIN", 256, 384), ap("TA"), ap("PS3", 256, 384), ALU.add)
+    outa(10)
+    outa(11)
+    small(T.ytrig, 1)
+    small(T.ysrc, 0)
+    store(10, 12)
+    small(T.ytg, 2)
+    outv(4)
+    outa(12)
+    store(3, 5)
+    outv(5)
+    outa(13)
+    store(12, 14)
+    outv(6)
+    store(5, 7)
+
+    for tok in stores:
+        wait("s", tok)
+    g.wait_ge(T.sem.sent, sent[0])
+    for s in ("qv", "qa", "qp", "qg"):
+        wait("g", (s, count[s]))

@@ -9,42 +9,52 @@ ZW = YC + M
 K = 16384.0
 CH = 512
 CFG = {
-    "x": [0, 1792, 3840, 5888, 7168],
-    "d": [0, 256, 640, 1024, 1664, 2048],
-    "dgv": 512,
-    "g10": "vvva", "y0": "vvva",
-    "g1": 640, "g2": 640, "g1l": 512, "g2l": 512, "g20": 0,
+    "x": [0, 2048, 4096, 6400, 7168],
+    "kb": 64,
+    "d": [0, 384, 1024, 1536, 2048],
+    "s": [0, 512, 1024, 1536, 2048], "sl": [0, 512, 1024, 1536, 2048],
+    "o": [0, 512, 1280, 2048, 2816, 3584, 4352, 5120, 5888, 6656, 7168],
+    "first": "li ov3 cv2 t0 t1 t3 t2 b1 b0 b3 b2 fa0 fa1 go gate0 oa0 oa1 oa2 sw ya1 tw pre1 tm cv3 s1 s0 gate1 ya0 bands2 c1 c4 c2 pk ss s3 s2 "
+             "D12 D01 c3 D34 D23 table firsts c5 c0 yv2 wa3 wa2 ya3 wv1 wv0 locm inv mg1 pre0 mg0 iv2 ia0 ia1 ia3 pre3 mg3 pre2 mg2 nh0+ tl0+",
+    "round": "m0 n1 nh1 d0 tl1 m1 d1 n0 pre0 nhb n3 n2 m2 u0 xp fl Aa0 fa0 d2 m3 sn idx u1 go0 d3 gb0 a2 a3 fa1 pre1 slot tm0 s0 ss0 gb1 gb2 "
+             "gb3 go1 s1 tm1 D01 s2 ss1 s3 Wa0 D12 D23 watch wa2 mg0 wv3 ia0 Ia1 pre2 iv1 mg1 mg2 pre3 D34 mg3 dd nh0+ tl0+",
+    "last": "m1 n0 nh1 d1 n1 m0 nhb d0 m2 xp n2 n3 tl1 fl d2 u0 sn idx Aa0 m3 fa0 u1 go0 pre1 pre0 d3 slot tm0 ss0 a2 gb0 s0 D01 a3 gb1 gb3 gb2 "
+            "fa1 go1 s1 tm1 D12 ss1 s3 s2 D24 Wa0 loc watch mg0 wv2 wa3 Ia1 Ia0 mg1 pre2 pre3 mg3 mg2 oa9+ oa1+ nh0+ nh1+ nhb+ oa7+ ov0+ ov2+ "
+            "ov8+ ov4+ ov3+ st0_1+ st9_10+ st1_3+ st7_9+ st3_5+ oa5+ trigs+ n1+ n0+ xp+ oa6+ swap+ st5_7+ srcs+ targets+",
 }
 
 SCRATCH = {
-    "Z": ("sbuf", [128, ZW], "bfloat16"), "LT": ("sbuf", [128, ZW], "bfloat16"),
+    "X": ("sbuf", [128, YC], "bfloat16"), "Z": ("sbuf", [128, ZW], "bfloat16"), "LT": ("sbuf", [128, ZW], "bfloat16"),
     "LO": ("sbuf", [128, RO * M], "bfloat16"), "LAND": ("sbuf", [128, RO * M], "bfloat16"),
     "MB": ("sbuf", [128, M], "bfloat16"), "DB": ("sbuf", [128, M], "bfloat16"), "AB": ("sbuf", [128, M], "bfloat16"),
     "GB": ("sbuf", [128, M], "bfloat16"), "IW": ("sbuf", [128, 16 + M], "bfloat16"), "I2": ("sbuf", [128, M], "bfloat16"),
-    "DG": ("sbuf", [128, M], "bfloat16"), "OUT": ("sbuf", [128, W], "bfloat16"),
+    "DG": ("sbuf", [128, M], "bfloat16"), "PK": ("sbuf", [128, W // 8], "bfloat16"),
+    "D1": ("dram", [128, W // 8], "bfloat16"), "D2": ("dram", [128, W // 8], "bfloat16"),
     "LI": ("sbuf", [128, 384], "int32"), "THI": ("sbuf", [128, 8], "int32"),
     "TAO": ("sbuf", [128, 128], "uint16"), "TAU": ("sbuf", [128, 128], "uint16"),
-    "S0U": ("sbuf", [128, 128], "uint16"), "TLU": ("sbuf", [128, 128], "uint16"), "SLU": ("sbuf", [128, 128], "uint16"),
-    "SSO": ("sbuf", [128, RO * 128], "uint16"), "SSI": ("sbuf", [128, RO * 128], "uint16"),
+    "STU": ("sbuf", [128, 256], "uint16"), "STI": ("sbuf", [128, 256], "uint16"), "SDO": ("sbuf", [128, 256], "float32"), "TLU": ("sbuf", [128, 128], "uint16"),
+    "SL": ("sbuf", [128, RO * 256], "uint16"), "SSI": ("sbuf", [128, RO * 128], "uint16"), "SSW": ("sbuf", [128, RO * 256], "uint16"),
     "LOC": ("sbuf", [128, 448], "uint16"), "INV": ("sbuf", [128, 128], "uint16"), "IDX": ("sbuf", [128, 128], "uint16"),
     "SA": ("sbuf", [128, 256], "float32"), "SB": ("sbuf", [128, 256], "float32"),
-    "TA": ("sbuf", [128, 128], "float32"), "DD": ("sbuf", [128, 128], "float32"), "TR": ("sbuf", [128, 256], "float32"),
+    "SDI": ("sbuf", [128, 256], "float32"), "TR": ("sbuf", [128, 384], "float32"),
     "U0": ("sbuf", [128, 256], "float32"), "U1": ("sbuf", [128, 256], "float32"), "SLOT": ("sbuf", [128, 256], "float32"),
-    "TM": ("sbuf", [128, 256], "float32"), "THR": ("sbuf", [128, 256], "float32"), "FIN": ("sbuf", [128, 384], "float32"),
+    "TM": ("sbuf", [128, 256], "float32"), "FIN": ("sbuf", [128, 384], "float32"),
     "NHB": ("sbuf", [128, 128], "bfloat16"), "XP": ("sbuf", [128, 128], "bfloat16"), "FL": ("sbuf", [128, 128], "bfloat16"),
     "C0": ("sbuf", [128, 128], "bfloat16"), "C1": ("sbuf", [128, 128], "bfloat16"), "SC": ("sbuf", [128, 128], "bfloat16"),
     "RI": ("sbuf", [128, 16], "int32"), "RJ": ("sbuf", [128, 16], "int32"), "RK": ("sbuf", [128, 8], "int32"),
-    "RL": ("sbuf", [128, 16], "float32"), "CL": ("sbuf", [128, 16], "float32"), "HM": ("sbuf", [128, 64], "float32"),
+    "RL": ("sbuf", [128, 16], "float32"), "CL": ("sbuf", [128, 16], "float32"), "HM": ("sbuf", [128, 80], "float32"),
     "RAMP": ("sbuf", [128, 128], "float32"), "KR": ("sbuf", [128, 128], "bfloat16"),
-    "ONE": ("sbuf", [128, 144], "float32"), "W32": ("sbuf", [128, 6 * 128], "float32"), "BG": ("sbuf", [128, 144], "float32"),
-    "WB": ("sbuf", [128, 9 * 128], "bfloat16"), "BB": ("sbuf", [128, 4 * 144], "bfloat16"),
+    "ONE": ("sbuf", [128, 128], "float32"), "W32": ("sbuf", [128, 3 * 128], "float32"),
+    "FB": ("sbuf", [128, 144 + 4 * 128], "bfloat16"),
+    "SEL": ("sbuf", [128, 32], "bfloat16"), "ET": ("sbuf", [128, 512], "bfloat16"), "NT": ("sbuf", [128, 128], "bfloat16"),
+    "WB": ("sbuf", [128, 12 * 128], "bfloat16"), "BB": ("sbuf", [128, 5 * 144], "bfloat16"),
 }
 for _b in range(8):
     SCRATCH["PS%d" % _b] = ("psum", [128, 512], "float32")
 
-NDMA = 20
-SEMAPHORES = (["qv", "qa", "qp", "qg", "sent", "ata"] + ["d%d" % i for i in range(NDMA)]
-              + ["as%d" % t for t in range(RO)] + ["al%d_%d" % (t, c) for t in range(RO) for c in range(4)])
+NDMA = 24
+SEMAPHORES = (["qv", "qa", "qp", "qg", "sent", "ata", "alt", "abk", "asc"] + ["d%d" % i for i in range(NDMA)]
+              + ["as%d_%d" % (t, p) for t in range(RO) for p in range(2)] + ["al%d_%d" % (t, c) for t in range(RO) for c in range(5)])
 
 
 def rank_program(g, core, T, topo):
@@ -52,11 +62,9 @@ def rank_program(g, core, T, topo):
     if rank is None:
         return
     dst = T.cores[(rank + 1) % len(T.cores)]
-    rid, pid, _ = topo.addr(dst)
-    emask = topo.mask(core, dst)
-    neng = len(topo.engines(core, dst))
     src_core = T.cores[(rank - 1) % len(T.cores)]
     nin = len(topo.engines(src_core, core))
+    nback = len(topo.engines(dst, core))
     odd = rank % 2
 
     Q = {"v": g.vector, "a": g.scalar, "p": g.tensor, "g": g, "s": g.sync}
@@ -118,18 +126,19 @@ def rank_program(g, core, T, topo):
         fn().then_inc(T.sem[s], 1)
         note(q, reads, writes, (s, count[s]))
 
-    def dma(q, out, in_, reads, writes):
-        order(q, reads, writes, ())
+    def dma(q, out, in_, reads, writes, ext=()):
+        order(q, reads, writes, ext)
         s = "d%d" % ndma[0]
         ndma[0] += 1
         Q[q].dma_start(out, in_).then_inc(T.sem[s], 16)
         note(q, reads, writes, (s, 16))
         return (s, 16)
 
-    def send(land, src, sem):
+    def send(land, src, sem, to=dst):
         order("g", [src], [], ())
-        g.remote_dma(land[3], src[3], T.sem[sem], T.sem.sent, pid, rid, emask)
-        sent[0] += neng
+        rid, pid, _ = topo.addr(to)
+        g.remote_dma(land[3], src[3], T.sem[sem], T.sem.sent, pid, rid, topo.mask(core, to))
+        sent[0] += len(topo.engines(core, to))
 
     def aps(*xs):
         return [x for x in xs if isinstance(x, tuple)]
@@ -155,6 +164,9 @@ def rank_program(g, core, T, topo):
         i0 = in_[3] if off is None else ind(in_, off)
         run("v", aps(in_, off), [out], lambda: g.vector.tensor_copy(out[3], i0), ext)
 
+    def fill(out, value):
+        run("v", [], [out], lambda: g.vector.memset(out[3], value))
+
     def act(out, in_, func=ACT.Identity, bias=0.0, scale=1.0, off=None, ext=()):
         i0 = in_[3] if off is None else ind(in_, off)
         run("a", aps(in_, bias, scale, off), [out],
@@ -179,8 +191,8 @@ def rank_program(g, core, T, topo):
         else:
             run("g", [], [out], lambda: g.iota(out[3], pattern, base, cm))
 
-    def sel(out, in_, pattern, cmp, fill, base, cm):
-        run("g", [in_], [out], lambda: g.affine_select(out[3], in_[3], pattern, cmp, fill, base, cm))
+    def sel(out, in_, pattern, cmp, value, base, cm):
+        run("g", [in_], [out], lambda: g.affine_select(out[3], in_[3], pattern, cmp, value, base, cm))
 
     def chunk(name, c, base=0, n=CH):
         return ap(name, base + c * n, base + (c + 1) * n)
@@ -194,120 +206,192 @@ def rank_program(g, core, T, topo):
     def lspan(name, a, b, base=0):
         return ap(name, base + a // 16, base + b // 16)
 
-    BF, BH, BL, BS = 0, 1, 2, 3
+    BF, BH, BL, BS, BN = 0, 1, 2, 3, 4
 
     def wrap(out, kind, name, a, b, start=True, stop=True):
         mm(out, [(ap("BB", kind * 144 + 15 - r, kind * 144 + 143 - r), ap(name, a + r, b, 16)) for r in range(16)], start, stop)
 
-    def band(kind, scale):
-        act(ap("BB", kind * 144, kind * 144 + 144), ap("BG"), scale=scale)
+    def pick(bank, base, name, a, d0, d1):
+        end, cols = base + 128 * (d1 - d0), ap("SEL", 8 * d0, 8 * d1)
 
-    I32, PM32, SWI, B32, W032, W132 = [ap("W32", i * 128, (i + 1) * 128) for i in range(6)]
-    IB, N16, DSG, PMB, NBK, W0, W1, KI, NKI = [ap("WB", i * 128, (i + 1) * 128) for i in range(9)]
-    HC, LC, M01, M23, WS, WL, H57, IC, SG, IN7, TH, NTH = [col("CL", j) for j in range(12)]
-    R4 = col("RL", 4)
-    ZX, ZA, LTX = ap("Z", 0, YC), ap("Z"), ap("LT", 0, YC)
-    XB, DBN = CFG["x"], CFG["d"]
+        def fn():
+            for r in range(16):
+                ins = g.tensor.matmul(T[bank][:, base + r:end:16], T[name][:, a + r:a + M:16], cols[3], True, True)
+            return ins
+        run("p", [ap(name, a, a + M), cols], [ap(bank, base, end)], fn)
+
+    def turned(out, a, more=(), start=True, stop=True):
+        mm(out, [(ap("ET", a, a + 128), I128), (ap("ET", a + 128, a + 256), IB)] + list(more), start, stop)
+
+    def band(kind, scale):
+        act(ap("BB", kind * 144, kind * 144 + 144), ap("BB", 0, 144), scale=scale)
+
+    I32, PM32, SWI = [ap("W32", i * 128, (i + 1) * 128) for i in range(3)]
+    IB, N16, DSG, PMB, NBK, W0, W1, NW0, KI, NKI, BK, I128 = [ap("WB", i * 128, (i + 1) * 128) for i in range(12)]
+    ONES, ONEB = ap("FB", 0, 144), ap("FB", 0, 128)
+    FK, FNK, F16, FSG = [ap("FB", 144 + i * 128, 272 + i * 128) for i in range(4)]
+    WS, WL, IC, SG, IN7, TH, PH, PL, PB = [col("CL", j) for j in range(9)]
+    R4, HC, LC = col("RL", 4), col("RL", 2), col("RL", 10)
+    XX, ZX, ZA, LTX = ap("X"), ap("Z", 0, YC), ap("Z"), ap("LT", 0, YC)
+    XB, DBN, kb = CFG["x"], CFG["d"], CFG["kb"]
+    KP = [0, kb, 128]
+    EP = [0, 16 * kb, M]
+    HP, EH = [0, 64, 128], [0, M // 2, M]
+
+    def half(name, h, base=0):
+        return ap(name, base + HP[h], base + HP[h + 1])
+
+    def shalf(name, h, base=0):
+        return half(name, h, base + (128 * h if kb == 64 else 0))
+
+    def part(name, p, base=0):
+        return ap(name, base + KP[p], base + KP[p + 1])
+
+    def wide(name, p, base=0):
+        return ap(name, base + 2 * KP[p], base + 2 * KP[p + 1])
+
+    def cpart(name, p, base=0):
+        return part(name, p, base + kb)
+
+    def spart(name, p, base=0):
+        return part(name, p, base + 128 * p)
+
+    def call(name, base=0):
+        return ap(name, base + kb, base + kb + 128)
+
+    def twice(name, base, mat, src):
+        for p in range(2):
+            if KP[p] < KP[p + 1]:
+                mm(spart(name, p, base), [(mat, part(src, p))])
+        mm(call(name, base), [(mat, ap(src))])
 
     TG, SRC, TRG = ap("LI", 0, 128), ap("LI", 128, 256), ap("LI", 256, 384)
     dma("s", TG[3], T.tg[:], [], [TG])
+    dma("s", SRC[3], T.src[:], [], [SRC])
+    dma("s", TRG[3], T.trig[:], [], [TRG])
     for c in range(len(XB) - 1):
-        z = span("Z", XB[c], XB[c + 1], PAD)
+        z = span("X", XB[c], XB[c + 1], PAD)
         dma("s", z[3], T.x[:, XB[c]:XB[c + 1]], [], [z])
-    dma("a", SRC[3], T.src[:], [], [SRC])
-    dma("a", TRG[3], T.trig[:], [], [TRG])
-    dma("a", col("THI", 0)[3], T.th[:], [], [col("THI", 0)])
+    dma("s", col("THI", 0)[3], T.th[:], [], [col("THI", 0)])
 
     iota(ap("RI"), [[-1, 16]], 16, 1, False)
     iota(ap("RAMP"), [[1, 128]], 0, 0)
-    iota(ap("ONE"), [[0, 144]], 1, 0)
-    one = ap("ONE", 0, 128)
-    sel(ap("BG"), ap("ONE"), [[0, 9], [1, 16]], ALU.is_equal, 0.0, -15, 0)
-    sel(I32, one, [[-1, 128]], ALU.is_equal, 0.0, 0, 1)
-    run("v", [], [ap("Z", 0, PAD)], lambda: g.vector.memset(T.Z[:, 0:PAD], 0.0))
+    fill(ONES, 1.0)
+    fill(ap("X", 0, PAD), 0.0)
+    fill(ap("C1", 0, 64), -16.0 if odd else -1.0)
+    bf = ap("BB", 0, 144)
+    sel(bf, ONES, [[0, 9], [1, 16]], ALU.is_equal, 0.0, -15, 0)
+    sel(bf, bf, [[-16, 9], [0, 16]], ALU.is_ge, 0.0, 0, 1)
+    sel(bf, bf, [[16, 9], [0, 16]], ALU.is_ge, 0.0, 15, -1)
+    sel(IB, ONEB, [[-1, 128]], ALU.is_equal, 0.0, 0, 1)
     ts(ap("RJ"), ap("RI"), 15, None, ALU.bitwise_and)
-    run("v", [], [ap("C1")], lambda: g.vector.memset(T.C1[:], 0.0))
+    fill(ap("Z", 0, PAD), 0.0)
     ts(ap("RL"), ap("RJ"), 0.0, None, ALU.is_equal)
-    tt(ap("CL", 0, 2), ap("RL", 0, 2), ap("RL", 2, 4), ALU.add)
-    tt(ap("CL", 2, 4), ap("RL", 0, 4, 2), ap("RL", 1, 4, 2), ALU.add)
-    ts(ap("LT", 0, 128), ap("RAMP"), LC, None, ALU.mult)
-    ts(ap("HM"), ap("RAMP", 0, 64), HC, None, ALU.mult)
-    ts(H57, col("RL", 2), float(YC // 128), None, ALU.mult)
+    cp(IC, col("RJ", 0))
+    act(PH, IC, ACT.Sign, bias=7.5, scale=-1.0)
+    act(PL, PH, bias=0.5, scale=-0.5)
+    act(PH, PH, bias=0.5, scale=0.5)
+    act(PB, IC, bias=1.0, scale=7.0)
+    act(PB, PB, scale=PH)
+    act(ap("CL", 9, 12), ap("RAMP", 1, 4), scale=PH)
+    act(col("CL", 11), PH, scale=4.0)
+    act(ap("PK", 0, 128), ap("RAMP"), bias=PB, scale=PL)
+    act(WL, HC, bias=LC, scale=128.0)
+    act(IN7, col("RL", 0), scale=7.0)
+    band(BL, WL)
+    act(ap("BB", BN * 144, BN * 144 + 144), ap("BB", BL * 144, BL * 144 + 144), scale=-1.0)
+    HY = YC // 128
+    ts(ap("HM", 0, 16), ap("RAMP", 0, 16), HC, None, ALU.mult)
+    ts(ap("HM", 16, 80), ap("RAMP", 0, 64), float(-HY), HC, ALU.add, ALU.mult)
+    ts(col("CL", 15), HC, float(HY), None, ALU.mult)
+    ts(ap("LT", YC, YC + 128), ap("RAMP"), LC, col("CL", 15), ALU.mult, ALU.add)
     n = 128
-    while n < 2048:
-        ts(ap("LT", n, 2 * n), ap("LT", 0, n), col("HM", n // 128), None, ALU.add)
+    while n < M:
+        ts(ap("LT", YC + n, YC + 2 * n), ap("LT", YC, YC + n), col("HM", n // 128), None, ALU.add)
         n *= 2
+    act(ap("LT", 0, M), ap("LT", YC, ZW), bias=col("HM", 16))
+    ts(ap("LT", 3 * M, YC), ap("LT", YC, YC + YC - 3 * M), col("HM", 64), None, ALU.add)
     ts(ap("TAO"), TG, float(PAD), None, ALU.add)
     send(ap("TAU"), ap("TAO"), "ata")
     ATA = [("ata", nin)]
-    act(ap("LT", YC, ZW), ap("LT", 0, M), bias=H57, scale=M23)
-    ts(ap("LT", 2048, 4096), ap("LT", 0, 2048), col("HM", 16), None, ALU.add)
-    ts(ap("LT", 4096, YC), ap("LT", 0, YC - 4096), col("HM", 32), None, ALU.add)
+    ts(ap("LT", 2 * M, 3 * M), ap("LT", YC, ZW), col("HM", 48), None, ALU.add)
+    ts(ap("STU"), ap("LI", 128, 384), float(PAD), None, ALU.add)
+    send(ap("STI"), ap("STU"), "abk", src_core)
+    ts(ap("LT", M, 2 * M), ap("LT", YC, ZW), col("HM", 32), None, ALU.add)
+    act(col("LT", 0), R4)
+    run("v", [ap("LT", YC, ZW), ap("TAO")], [LTX], lambda: g.vector.tensor_copy(ind(LTX, ap("TAO")), T.LT[:, YC:ZW]))
+    rows = [T.LT[j:128:8, PAD:YC] for j in (0, 2)]
+    LTR = ap("LT", PAD, YC)
+    dma("s", T.D1[:], rows[1], [LTR], [ap("D1")])
 
-    sel(ap("BG"), ap("BG"), [[-16, 9], [0, 16]], ALU.is_ge, 0.0, 0, 1)
-    sel(B32, one, [[-16, 8], [0, 16]], ALU.is_ge, 0.0, 0, 1)
-    sel(ap("BG"), ap("BG"), [[16, 9], [0, 16]], ALU.is_ge, 0.0, 15, -1)
-    sel(B32, B32, [[16, 8], [0, 16]], ALU.is_ge, 0.0, 15, -1)
-    sel(PM32, one, [[-2, 64], [0, 2]], ALU.is_ge, 0.0, 0, 1)
-    sel(W032, B32, [[-1, 128]], ALU.is_ge, 0.0, 0, 1)
-    sel(W132, B32, [[-2, 64], [1, 2]], ALU.is_ge, 0.0, -1, 1)
-    sel(W032, W032, [[-1, 128]], ALU.not_equal, float(CAP + 8), 0, 1)
-    sel(PM32, PM32, [[2, 64], [0, 2]], ALU.is_ge, 0.0, 1, -1)
-    sel(W132, W132, [[-2, 64], [1, 2]], ALU.not_equal, float(CAP + 8), -1, 1)
-    iota(ap("KR"), [[-1, 128]], 0, 0)
-    sel(SWI, PM32, [[-1, 128]], ALU.not_equal, -1.0, 0, 1)
+    def blocks(out, in_, n):
+        sel(out, in_, [[-n, 128 // n], [0, n]], ALU.is_ge, 0.0, 0, 1)
+        sel(out, out, [[n, 128 // n], [0, n]], ALU.is_ge, 0.0, n - 1, -1)
+
+    def diag(out, in_):
+        sel(out, in_, [[-1, 128]], ALU.is_equal, 0.0, 0, 1)
+
+    def later(out, in_, pattern, base, value):
+        sel(out, in_, pattern, ALU.is_ge, 0.0, base, 1)
+        sel(out, out, pattern, ALU.not_equal, value, base, 1)
+
+    iota(FK, [[0, 128]], int(K), 0)
+    blocks(BK, FK, 16)
+    later(W0, BK, [[-1, 128]], 0, K * (CAP + 8))
+    iota(FNK, [[0, 128]], int(-K), 0)
+    blocks(NBK, FNK, 16)
+    iota(F16, [[0, 128]], -16, 0)
+    diag(N16, F16)
+
+    def exchange():
+        sel(SWI, ap("ONE"), [[-2, 64], [1, 2]], ALU.is_equal, 0.0, -1, 1)
+        sel(SWI, SWI, [[-1, 128]], ALU.not_equal, -1.0, 0, 1)
+
+    later_ones = {
+        "c6": lambda: (sel(ap("SEL"), ap("FB", 0, 32), [[-2, 2], [-8, 2], [-16, 8]], ALU.is_equal, 0.0, 0, 1),
+                       iota(I128, [[0, 128]], 128, 0), diag(I128, I128)),
+        "c0": lambda: (blocks(PMB, ONEB, 2), diag(KI, FK)),
+        "c1": lambda: (iota(FSG, [[0, 64], [-2, 2]], 1, 0), diag(DSG, FSG), iota(ap("KR"), [[-1, 128]], 0, 0)),
+        "c2": lambda: (iota(ap("ONE"), [[0, 128]], 1, 0), exchange()),
+        "c3": lambda: later(W1, BK, [[-2, 64], [1, 2]], -1, K * (CAP + 8)),
+        "c4": lambda: later(NW0, NBK, [[-1, 128]], 0, -K * (CAP + 8)),
+        "c5": lambda: (diag(I32, ap("ONE")), diag(NKI, FNK)),
+    }
 
     cm, cb = (-1.0, 16.0) if odd else (1.0, 1.0)
+    om, ob = (-1.0, 16.0) if odd else (1.0, -1.0)
 
     def conv(q, c):
-        z = span("Z", XB[c], XB[c + 1], PAD)
+        x, z = span("X", XB[c], XB[c + 1], PAD), span("Z", XB[c], XB[c + 1], PAD)
         if q == "v":
-            ts(z, z, cm, cb, ALU.mult, ALU.add)
+            ts(z, x, cm, cb, ALU.mult, ALU.add)
         else:
-            act(z, z, bias=cb, scale=cm)
+            act(z, x, bias=cb, scale=cm)
 
-    S = [ap("SA"), ap("SB")]
-
-    def sl(i):
-        return ap(S[i][0], 0, 128)
-
-    def ss(i):
-        return ap(S[i][0], 128, 256)
-
-    T1P, TL = ap("PS2", 0, 128), ap("PS2", 128, 256)
-    dv = M - CFG["dgv"]
+    S = ["SA", "SB"]
+    T1P, TL = ("PS2", 0), ("PS2", 128)
+    n = 128
+    while n < W // 8:
+        m = min(n, W // 8 - n)
+        act(ap("PK", n, n + m), ap("PK", 0, m), bias=col("CL", 9 + n // 256))
+        n *= 2
     conv("a", 0)
-    ts(ap("CL", 4, 6), ap("RL", 0, 4, 2), 128.0, None, ALU.mult)
-    ts(col("RK", 0), col("RJ", 0), 1, None, ALU.bitwise_and)
-    cp(IC, col("RJ", 0))
-    tt(ap("CL", 4, 6), ap("CL", 4, 6), ap("RL", 1, 4, 2), ALU.add)
-    ts(SG, col("RK", 0), -2.0, 1.0, ALU.mult, ALU.add)
-    ts(IN7, col("RL", 0), 7.0, None, ALU.mult)
-    cp(TH, col("THI", 0))
-    ts(NTH, col("THI", 0), -1.0, None, ALU.mult)
-    act(IB, I32)
-    act(span("DG", 0, dv), LTX, scale=M01, off=lspan("TAU", 0, dv), ext=ATA)
-    conv("v", 1)
-    ts(ss(0), SRC, float(PAD), None, ALU.add)
-    ts(ap("S0U"), SRC, float(PAD), None, ALU.add)
-    ts(ap("TR", 0, 128), TRG, float(PAD), None, ALU.add)
-    ts(ap("TLU"), TRG, float(PAD), None, ALU.add)
-    cp(ap("TA"), TG)
-    ts(ap("IW", 0, 16), ap("Z", 0, 16), R4, None, ALU.add)
-    conv("v", 2)
-    ts(span("DG", dv, M), LTX, M01, None, ALU.mult, off=lspan("TAU", dv, M), ext=ATA)
-    cp(col("LT", 0), R4)
-    run("v", [ap("DG"), ap("LT", YC, ZW), ap("TAU")], [LTX],
-        lambda: g.vector.tensor_tensor(ind(LTX, ap("TAU")), T.DG[:], T.LT[:, YC:ZW], ALU.add), ATA)
-    band(BF, 1.0)
-    conv("a", 3)
+    conv("a", 1)
 
-    FAR = [ap("PS0", 0, 64), ap("PS0", 64, 128), ap("PS0", 0, 128)]
-    NH, VV, F2 = ap("PS4", 0, 128), ap("PS4", 128, 256), ap("PS4", 256, 512)
+    FB = ["PS6", "PS7"]
+    NH = ap("PS4", 0, 128)
     PAIR, IXP, SWP = ap("PS3", 0, 128), ap("PS3", 128, 256), ap("PS3", 256, 512)
-    QB = [ap("PS6"), ap("PS7"), ap("PS0"), ap("PS1")]
+    QB = ["PS0", "PS1"] + (["PS7"] if kb == 128 else [])
+    nq = len(QB)
+    TB = [ap("PS0"), ap("PS1"), ap("PS3"), ap("PS5")]
     FL = ap("FL")
     gs, gb = (-16.0, 144.0) if odd else (16.0, -128.0)
+
+    def far(p):
+        return ap(FB[p], 0, KP[p + 1] - KP[p])
+
+    def farh(h):
+        return far(h) if kb == 64 else half(FB[0], h)
 
     def flips(t):
         if t == 1:
@@ -315,217 +399,435 @@ def rank_program(g, core, T, topo):
         else:
             tt(FL, FL, ap("XP"), ALU.is_equal)
 
-    def watch(t):
-        mm(ap("PS3", 256, 384), [(I32, ap("TR", 0, 128))] + ([(I32, ap("TR", 128, 256))] if t > 1 else []) + [(KI, ap("NHB"))])
-        mm(ap("PS3", 384, 512), [(I32, ss((t + 1) % 2)), (NKI, ap("NHB"))])
-
-    def watch2(shift):
+    def watch(t, shift):
+        both = [(I32, ap("TR", 0, 128)), (I32, ap("TR", 128, 256))] if t > 1 else [(I32, ap("TR", 256, 384))]
+        mm(ap("PS3", 256, 384), both + [(KI, ap("NHB"))])
+        for h in range(2):
+            mm(half("PS3", h, 384), [(I32, shalf(S[(t + 1) % 2], h) if t > 1 else half("TR", h, 128)), (NKI, half("NHB", h))])
         act(ap("TR", 0, 128), ap("PS3", 256, 384), ACT.Relu, bias=shift - K)
         act(ap("TR", 128, 256), ap("PS3", 384, 512), ACT.Relu, bias=shift)
 
-    def lower(t, c):
-        mm(QB[c], [(N16, chunk("LAND", c, t * M))], False, True, ext=[("al%d_%d" % (t, c), nin)])
+    def amended(t):
+        st = {}
 
-    def merge(t, c):
-        tt(chunk("Z", c, YC), chunk("LAND", c, t * M), QB[c], ALU.max, ext=[("al%d_%d" % (t, c), nin)])
+        def hits():
+            act(ap("NHB"), NH)
+            mm(PAIR, [(PMB, ap("NHB"))])
 
-    def gate0(c):
-        ts(chunk("GB", c, 0, 1024), chunk("Z", c, PAD + P, 1024), 8.5, 16.0, ALU.is_lt if odd else ALU.is_gt, ALU.mult)
+        def kn():
+            for a in (256, 384):
+                mm(ap("PS4", a, a + 128), [(ap("NT"), KI)])
 
-    for t in range(RO):
-        cur, old = t % 2, (t + 1) % 2
-        last = t == RO - 1
+        st["x1"] = lambda: pick("PS6", 0, "I2", 0, 0, 4)
+        st["xv"] = lambda: ts(ap("NT"), ap("PS6", 256, 384), 0.0, None, ALU.is_equal)
+        st["xa"] = lambda: act(ap("NT"), ap("PS6", 256, 384), ACT.Relu, bias=1.0, scale=-1.0)
+        st["x2"] = lambda: mm(NH, [(ap("NT"), IB)])
+        st["Ea"] = lambda: act(ap("ET"), ap("PS6"))
+        st["Ev"] = lambda: cp(ap("ET"), ap("PS6"))
+        st["Es"] = lambda: act(ap("ET", 0, 256), ap("PS6", 0, 256))
+        st["x3"] = lambda: turned(ap("PS5", 0, 128), 0)
+        st["x4"] = lambda: turned(ap("PS5", 128, 256), 256)
+        st["hb"], st["kn"] = hits, kn
+        return st
+
+    def plan(t):
+        return CFG["first" if t == 0 else "last" if t == RO - 1 else "round"].split()
+
+    def steps(t):
+        cur, old = S[t % 2], S[(t + 1) % 2]
         win = ZX if t == 0 else ZA
-        if t == 0:
-            tb = [ap("PS6"), ap("PS7"), ap("PS5"), ap("PS3")]
-            for c in range(4):
-                act(chunk("DB", c), ZX, scale=-1.0, off=lst("TLU", c))
-                mm(tb[c], [(IB, chunk("Z", c, PAD + P)), (IB, chunk("DB", c))])
-                if c > 0:
-                    act(chunk("AB", c - 1), tb[c - 1], ACT.Abs)
-                if c == 2:
-                    wrap(FAR[0], BF, "AB", 0, 1024)
-            act(NBK, B32, scale=-K)
-            act(chunk("AB", 3), tb[3], ACT.Abs)
-            wrap(FAR[1], BF, "AB", 1024, 2048)
-            act(W0, W032, scale=K)
-            band(BL, WL)
-            gate0(0)
-            ts(ap("C0"), FAR[2], TH, None, ALU.is_lt)
-        else:
-            nd = len(DBN) - 1
-            wrap(ap("PS5", 0, 128), BL, "I2", 0, M)
-            for c in range(nd):
-                gather("a", span("MB", DBN[c], DBN[c + 1]), ZA, lspan("LOC", DBN[c], DBN[c + 1], P // 16))
-                if c == 0:
-                    act(ap("NHB"), NH)
-                    mm(PAIR, [(PMB, ap("NHB"))])
-                if c == 1:
-                    act(ap("XP"), PAIR, ACT.Abs, bias=-1.0)
-            wrap(ap("PS5", 128, 256), BS, "I2", 0, M)
-            for c in range(nd):
-                a, b = DBN[c], DBN[c + 1]
-                tt(span("DB", a, b), win, span("MB", a, b), ALU.subtract, off=lspan("TLU", a, b))
-                if c == 1:
-                    flips(t)
-                    mm(IXP, [(N16, ap("KR")), (DSG, FL)])
-                    mm(ap("PS4", 256, 384), [(IB, FL)])
-                    mm(ap("PS4", 384, 512), [(IB, FL)])
-                    act(ap("THR", 0, 128), FL, bias=TH, scale=NTH)
-                    act(ap("THR", 128, 256), FL, scale=TH)
-                if b == 1024:
-                    wrap(FAR[0], BF, "DB", 0, 1024, True, False)
-                if c == 2:
-                    ts(ap("IDX"), IXP, IC, None, ALU.add)
-                if b <= 1024:
-                    ts(span("AB", a, b), span("DB", a, b), 0.0, -2.0, ALU.min, ALU.mult)
-                else:
-                    act(span("AB", a, b), span("DB", a, b), ACT.Abs)
-                if b == 1024:
-                    wrap(FAR[0], BF, "AB", 0, 1024, False, True)
-            wrap(FAR[1], BF, "AB", 1024, 2048)
-            for c in range(4):
-                act(chunk("GB", c), ap("MB"), ACT.Relu, bias=gb, scale=gs, off=lst("IDX", c))
-            tt(ap("U0", 0, 128), sl(old), NH, ALU.mult)
-            tt(ap("U0", 128, 256), ss(old), NH, ALU.mult)
-            tt(S[cur], ap("U0"), ap("PS5", 0, 256), ALU.add)
-            tt(ap("U1"), S[cur], F2, ALU.mult)
-            mm(SWP, [(SWI, ap("U1"))])
-            tt(ap("C0"), FAR[2], ap("THR", 0, 128), ALU.is_lt)
-            tt(ap("C1"), FAR[2], ap("THR", 128, 256), ALU.is_lt)
-        mm(VV, [(W0, ap("C0"))] + ([(W1, ap("C1"))] if t > 0 else []), True, False)
-        run("v", [ap("C0"), ap("C1"), IN7], [ap("SC")],
-            lambda: g.vector.tensor_tensor_scan(T.SC[:], T.C0[:], T.C1[:], IN7[3], ALU.add, ALU.add))
-        mm(VV, [(NBK, ap("SC"))], False, True)
-        sso = ap("SSO", t * 128, (t + 1) * 128)
-        if t == 0:
-            wrap(ap("PS6", 0, 448), BL, "LT", PAD, YC)
-            tt(ap("TM", 128, 256), ss(0), VV, ALU.min)
-            cp(sso, ap("TM", 128, 256))
-            gate0(1)
-            slu = ("SSO", t * 128)
-        else:
-            tt(ap("SLOT", 128, 256), ss(cur), ap("PS3", 384, 512), ALU.add)
-            tt(ap("SLOT", 0, 128), sl(cur), ap("PS3", 256, 384), ALU.add)
-            tt(ap("TM", 128, 256), ap("SLOT", 128, 256), VV, ALU.min)
-            tt(ap("TM", 0, 128), ap("SLOT", 0, 128), VV, ALU.min)
-            cp(sso, ap("TM", 128, 256))
-            cp(ap("SLU"), ap("TM", 0, 128))
-            slu = ("SLU", 0)
-        send(ap("SSI", t * 128, (t + 1) * 128), sso, "as%d" % t)
-        for c in range(4):
-            tt(chunk("LO", c, t * M), win, chunk("GB", c), ALU.min, off=lst(slu[0], c, slu[1]))
-            send(chunk("LAND", c, t * M), chunk("LO", c, t * M), "al%d_%d" % (t, c))
-        AS = [("as%d" % t, nin)]
-        if t == 0:
-            act(ap("DG"), LTX, off=ap("S0U"))
-            wrap(ap("PS5", 0, 128), BL, "DG", 0, M)
-            act(N16, I32, scale=-16.0)
-            band(BH, R4)
-            band(BS, WS)
-            act(DSG, I32, scale=SG)
-            act(PMB, PM32)
-            act(W1, W132, scale=K)
-            act(KI, I32, scale=K)
-            act(NKI, I32, scale=-K)
-            act(ap("MB"), LTX, off=ap("TLU"))
-            act(sl(0), ap("PS5", 0, 128))
-            wrap(ap("PS5", 128, 256), BL, "MB", 0, M)
-            cp(ap("LOC"), ap("PS6", 0, 448))
-            ts(ap("INV"), ap("PS6", P // 16, 448), float(16 - YC), None, ALU.add)
-            for c in range(4):
-                gather(CFG["g10"][c], chunk("IW", c, 16), LTX, lst("SSI", c, t * 128), AS)
-            for c in range(4):
-                gather(CFG["y0"][c], chunk("Z", c, YC), ZX, lst("TAU", c))
-            tt(ap("DD"), ap("PS5", 128, 256), sl(0), ALU.subtract)
-            v = M - CFG["g20"]
-        else:
-            watch(t)
-            watch2(0.0)
-            v = M - CFG["g1l" if last else "g1"]
-            gather("a", span("IW", 0, v, 16), LTX, lspan("SSI", 0, v, t * 128), AS)
-            gather("v", span("IW", v, M, 16), LTX, lspan("SSI", v, M, t * 128), AS)
-            if not last:
-                tt(ap("DD"), TL, sl(cur), ALU.subtract)
-            v = M - CFG["g2l" if last else "g2"]
-        for q, a, b in (("a", 0, 1024), ("a", 1024, v), ("v", v, M)):
+        w0, l0 = t * 256, t * 128
+        SB = CFG["sl" if t == RO - 1 else "s"]
+        st = {}
+
+        def dist0(c):
+            act(chunk("DB", c), XX, scale=-1.0, off=lst("STU", c, 128))
+            mm(TB[c], [(IB, chunk("X", c, PAD + P)), (IB, chunk("DB", c))])
+
+        def dist(c):
+            a, b = DBN[c], DBN[c + 1]
+            act(span("DB", a, b), ZA, scale=-1.0, off=lspan("TLU", a, b))
+            mm(ap(QB[c % 2], 0, b - a), [(IB, span("MB", a, b)), (IB, span("DB", a, b))])
+
+        def begin(q, c, n=CH):
+            if q == "v":
+                ts(chunk("Z", c, YC, n), XX, cm, cb, ALU.mult, ALU.add, off=lst("TAU", c, 0, n), ext=ATA)
+            else:
+                act(chunk("Z", c, YC, n), XX, bias=cb, scale=cm, off=lst("TAU", c, 0, n), ext=ATA)
+
+        def gate(h):
+            ts(span("GB", EH[h], EH[h + 1]), span("X", EH[h], EH[h + 1], PAD + P), 7.5, 16.0, ALU.is_gt, ALU.mult)
+
+        def size(q, a, b):
+            zero = 0.0 if t else cb
+            if q == "v":
+                ts(span("AB", a, b), span("DB", a, b), zero, -2.0, ALU.min, ALU.mult)
+            else:
+                act(span("AB", a, b), span("DB", a, b), ACT.Abs, bias=-zero)
+
+        begun = [False, False]
+
+        def total(h, name):
+            o = farh(h) if t else half(FB[0], h)
+            wrap(o, BF, name, EH[h], EH[h + 1], not begun[h], name == "AB")
+            if name == "DB" and t == 0:
+                mm(o, [(N16, ap("C1", 0, 64))], False, False)
+            begun[h] = True
+
+        def numbering():
+            cp(TH, col("THI", 0))
+            ts(ap("TR", 128, 384), ap("LI", 128, 384), float(PAD), None, ALU.add)
+
+        def go0():
+            ts(ap("C0"), ap(FB[0], 0, 128), TH, None, ALU.is_lt)
+            run("v", [ap("C0"), IN7], [ap("SC")], lambda: g.vector.tensor_tensor_scan(T.SC[:], T.C0[:], T.C0[:], IN7[3], ALU.add, ALU.max))
+            mm(ap(FB[0], 128, 256), [(W0, ap("C0")), (NBK, ap("SC"))])
+
+        def lists0():
+            tt(ap("TM", 0, 128), ap("TR", 128, 256), ap(FB[0], 128, 256), ALU.min)
+            cp(ap("SL", 0, 128), ap("TM", 0, 128))
+
+        def kept():
+            if t > 1:
+                tt(ap("U0"), ap(old), ap("PS4", 256, 512), ALU.min)
+                return
+            for h in range(2):
+                tt(shalf("U0", h), half("TR", h, 128), shalf("PS4", h, 256), ALU.min)
+            tt(call("U0"), ap("SDI", 0, 128), call("PS4", 256), ALU.min, ext=[("asc", nin)])
+
+        def table():
+            dma("s", rows[0], T.PK[:], [ap("PK")], [LTR])
+            mine = hist["LT"].pop()
+            dma("s", rows[1], T.D2[:], [], [LTR], [("alt", nin)])
+            hist["LT"].append(mine)
+
+        def go(p):
+            c0, c1, sc = part("C0", p), part("C1", p), part("SC", p)
+            ini = IN7 if p == 0 else col("SC", kb - 1)
+            ts(c0, far(p), TH, None, ALU.is_lt)
+            run("v", [c0, ini], [sc], lambda: g.vector.tensor_tensor_scan(sc[3], c0[3], c0[3], ini[3], ALU.add, ALU.max))
+            n = KP[p + 1] - KP[p]
+            tt(c1, c0, part("FL", p), ALU.mult)
+            for j in range(2):
+                mm(ap(FB[p], 128 + j * n, 128 + (j + 1) * n), [(W0, c0), (NBK, sc), (W1, c1), (NW0, c1)])
+
+        def lists(p):
+            n = KP[p + 1] - KP[p]
+            tt(wide("TM", p), wide("SLOT", p), ap(FB[p], 128, 128 + 2 * n), ALU.min)
+            cp(wide("SL", p, w0), wide("TM", p))
+
+        def numbers(c):
+            a, b = SB[c], SB[c + 1]
+            tt(span("LO", a, b, t * M), win, span("GB", a, b), ALU.min, off=lspan("SL", a, b, w0 + kb if t else 0))
+
+        def numbers_a(c):
+            a, b = SB[c], SB[c + 1]
+            act(span("DB", a, b), win, scale=-1.0, off=lspan("SL", a, b, w0 + kb))
+            mm(ap("PS4", 0, b - a), [(IB, span("DB", a, b)), (IB, span("GB", a, b))])
+
+        def out(a, b):
+            send(span("LAND", SB[a], SB[b], t * M), span("LO", SB[a], SB[b], t * M), "al%d_%d" % (t, a))
+
+        piece = {}
+        for name in plan(t):
+            if name[0] == "D":
+                a, b = int(name[1]), int(name[2])
+                st[name] = lambda a=a, b=b: out(a, b)
+                piece.update({c: a for c in range(a, b)})
+
+        def look(q, a, b, p):
+            if "ssW" in plan(t):
+                gather(q, span("IW", a, b, 16), LTX, lspan("SSW", a, b, w0 + 128 * p), [("as%d_0" % t, nin)])
+            elif a < b:
+                gather(q, span("IW", a, b, 16), LTX, lspan("SSI", a, b, l0), [("as%d_%d" % (t, p if t else 0), nin)])
+
+        def turn(q, a, b):
             if a < b:
                 gather(q, span("I2", a, b), ap("IW"), lspan("INV", a, b))
+
+        def merge(c):
+            al = [("al%d_%d" % (t, piece[c]), nin)]
+            a, b = SB[c], SB[c + 1]
+            mm(ap(QB[c % nq], 0, b - a), [(N16, span("LAND", a, b, t * M))], False, True, ext=al)
+            tt(span("Z", a, b, YC), span("LAND", a, b, t * M), ap(QB[c % nq], 0, b - a), ALU.max, ext=al)
+
+        def trig(a, b, s):
+            tt(span("PS2", a, b), span("SDI", a, b, 128), span("PS4", a, b), ALU.mult, ext=[("asc", nin)])
+            tt(span("PS2", a, b, 128), span("PS2", a, b), span("SDI", a, b) if t == 1 else span(s, a, b, kb), ALU.add)
+            cp(span("TLU", a, b), span("PS2", a, b, 128))
+
+        def nhb():
+            act(ap("NHB"), NH)
+            mm(PAIR, [(PMB, ap("NHB"))])
+            twice("PS4", 256, KI, "NHB")
+
+        def fl():
+            flips(t)
+            mm(IXP, [(N16, ap("KR")), (DSG, FL)])
+            twice("PS5", 256, IB, "FL")
+
+        def u1():
+            tt(ap("U1"), ap(cur), ap("PS5", 256, 512), ALU.mult)
+            mm(SWP, [(SWI, ap("U1"))])
+
+        def loc():
+            wrap(ap("PS6", 0, P // 16), BL, "LT", PAD, PAD + P)
+            cp(ap("LOC", 0, P // 16), ap("PS6", 0, P // 16))
+
+        def first(q, name, h, base):
+            gather(q, span(name, EH[h], EH[h + 1]), LTX, half("STI", h, base), [("abk", nback)])
+
+        def firsts():
+            act(ap("SDO"), ap("PS4", 0, 256))
+            send(ap("SDI"), ap("SDO"), "asc")
+
+        def wraps():
+            wrap(ap("PS4", 0, 128), BL, "DG", 0, M)
+            wrap(ap("PS4", 128, 256), BN, "DG", 0, M, True, False)
+
+        def inv():
+            cp(ap("LOC", P // 16, 448), ap("PS3", 0, 128))
+            ts(ap("INV"), ap("PS3", 0, 128), float(16 - YC), None, ALU.add)
+
+        def bands2():
+            act(WS, col("RL", 0), bias=col("RL", 8), scale=128.0)
+            band(BH, R4)
+            band(BS, WS)
+            act(ap("IW", 0, 16), ap("Z", 0, 16), bias=R4)
+
+        st["bands2"] = bands2
+        st.update(later_ones)
+
         for c in range(4):
-            mm(QB[c], [(IB, chunk("Z", c, YC))], True, False)
-        for c in range(3):
-            lower(t, c)
-            merge(t, c)
-        if last:
-            lower(t, 3)
-            merge(t, 3)
-            wrap(NH, BH, "I2", 0, M)
-            wrap(ap("PS5", 128, 256), BS, "I2", 0, M)
-        else:
-            wrap(ap("PS4", 0, 64), BH, "I2", 0, 1024)
-            lower(t, 3)
-            wrap(ap("PS4", 64, 128), BH, "I2", 1024, 2048)
-            merge(t, 3)
-            tt(T1P, ap("DD"), NH, ALU.mult)
-            tt(TL, T1P, sl(cur), ALU.add)
-            cp(ap("TLU"), TL)
+            st["t%d" % c] = lambda c=c: dist0(c)
+            st["b%d" % c] = lambda c=c: act(chunk("AB", c), TB[c], ACT.Abs)
+            st["v%d" % c] = lambda c=c: tt(chunk("DB", c), ZX, chunk("X", c, PAD + P), ALU.add if odd else ALU.subtract, off=lst("STU", c, 128))
+            st["bv%d" % c] = lambda c=c: size("v", c * CH, (c + 1) * CH)
+            st["ba%d" % c] = lambda c=c: size("a", c * CH, (c + 1) * CH)
+            st["cv%d" % c] = lambda c=c: conv("v", c)
+            st["ca%d" % c] = lambda c=c: conv("a", c)
+            st["gb%d" % c] = lambda c=c: act(chunk("GB", c), ap("MB"), ACT.Relu, bias=gb, scale=gs, off=lst("IDX", c))
+        for c in range(len(SB) - 1):
+            st["s%d" % c] = lambda c=c: numbers(c)
+            st["g%d" % c] = lambda c=c: act(span("GB", SB[c], SB[c + 1]), ap("MB"), ACT.Relu, bias=gb, scale=gs, off=lspan("IDX", SB[c], SB[c + 1]))
+            st["gc%d" % c] = lambda c=c: act(span("GB", SB[c], SB[c + 1]), ap("MB"), ACT.Relu, bias=16.0 - gb, scale=-gs,
+                                             off=lspan("IDX", SB[c], SB[c + 1]))
+            st["sa%d" % c] = lambda c=c: numbers_a(c)
+            st["sb%d" % c] = lambda c=c: act(span("LO", SB[c], SB[c + 1], t * M), ap("PS4", 0, SB[c + 1] - SB[c]), ACT.Relu, scale=-1.0)
+            st["pre%d" % c] = lambda c=c: mm(ap(QB[c % nq], 0, SB[c + 1] - SB[c]), [(IB, span("Z", SB[c], SB[c + 1], YC))], True, False)
+            st["mg%d" % c] = lambda c=c: merge(c)
+        for c in range(len(DBN) - 1):
+            st["m%d" % c] = lambda c=c: gather("a", span("MB", DBN[c], DBN[c + 1]), ZA, lspan("LOC", DBN[c], DBN[c + 1], P // 16))
+            st["d%d" % c] = lambda c=c: tt(span("DB", DBN[c], DBN[c + 1]), win, span("MB", DBN[c], DBN[c + 1]), ALU.subtract,
+                                           off=lspan("TLU", DBN[c], DBN[c + 1]))
+            st["a%d" % c] = lambda c=c: size("a", DBN[c], DBN[c + 1])
+            st["av%d" % c] = lambda c=c: size("v", DBN[c], DBN[c + 1])
+            st["e%d" % c] = lambda c=c: dist(c)
+            st["f%d" % c] = lambda c=c: act(span("AB", DBN[c], DBN[c + 1]), ap(QB[c % 2], 0, DBN[c + 1] - DBN[c]), ACT.Abs)
+        for p in range(2):
+            st["Av%d" % p] = lambda p=p: size("v", EH[p], EH[p + 1])
+            st["Aa%d" % p] = lambda p=p: size("a", EH[p], EH[p + 1])
+            st["GB%d" % p] = lambda p=p: act(span("GB", EH[p], EH[p + 1]), ap("MB"), ACT.Relu, bias=gb, scale=gs, off=half("IDX", p))
+            st["fd%d" % p] = lambda p=p: total(p, "DB")
+            st["fa%d" % p] = lambda p=p: total(p, "AB")
+            st["gate%d" % p] = lambda p=p: gate(p)
+            st["go%d" % p] = lambda p=p: go(p)
+            st["tm%d" % p] = lambda p=p: lists(p)
+            st["ss%d" % p] = lambda p=p: send(part("SSI", p, l0), spart("SL", p, w0), "as%d_%d" % (t, p))
+            st["nh%d" % p] = lambda p=p: wrap(half("PS4", p), BH, "I2", EH[p], EH[p + 1])
+            st["n%d" % p] = lambda p=p: wrap(half("PS5", p, kb), BL, "I2", EH[p], EH[p + 1])
+            st["n%d" % (p + 2)] = lambda p=p: wrap(shalf("PS5", p), BS, "I2", EH[p], EH[p + 1])
+            st["tl%d" % p] = lambda p=p: trig(HP[p], HP[p + 1], old)
+        st["tl"] = lambda: trig(0, 128, old)
+        st["li"], st["table"], st["go"], st["tm"], st["u0"] = numbering, table, go0, lists0, kept
+        st["ss"] = lambda: send(ap("SSI", 0, 128), ap("SL", 0, 128), "as0_0")
+        st["ssW"] = lambda: send(ap("SSW", w0, w0 + 256), ap("SL", w0, w0 + 256), "as%d_0" % t)
+        st["pk"] = lambda: send(ap("D2"), ap("D1"), "alt")
+        st["nhb"], st["fl"], st["u1"], st["loc"], st["inv"] = nhb, fl, u1, loc, inv
+        st["sw"], st["firsts"] = wraps, firsts
+        st["tw"] = lambda: wrap(ap("PS4", 128, 256), BL, "MB", 0, M, False, True)
+        st["xp"] = lambda: act(ap("XP"), PAIR, ACT.Abs, bias=-1.0)
+        st["idx"] = lambda: ts(ap("IDX"), IXP, IC, None, ALU.add)
+        st["sn"] = lambda: tt(ap(cur), ap("U0"), ap("PS5", 0, 256), ALU.add)
+        st["slot"] = lambda: tt(ap("SLOT"), ap(cur), SWP, ALU.add)
+        def kept_a():
+            for h in range(2):
+                mm(shalf("PS4", h, 256), [(I32, shalf(old, h) if t > 1 else half("TR", h, 128)), (KI, half("NHB", h))])
+            mm(call("PS4", 256), [(I32, call(old) if t > 1 else ap("SDI", 0, 128)), (KI, ap("NHB"))], ext=[("asc", nin)])
+            act(ap("U0"), ap("PS4", 256, 512), ACT.Relu, bias=-K)
 
-    om, ob = (-1.0, 16.0) if odd else (1.0, -1.0)
-    cur = (RO - 1) % 2
+        def hits_a():
+            act(ap("NHB"), NH)
+            mm(PAIR, [(PMB, ap("NHB"))])
 
-    def outv(c):
-        ts(chunk("OUT", c), ZA, om, ob, ALU.mult, ALU.add, off=lst("LOC", c))
+        def u1_a():
+            tt(ap("U1"), ap(cur), ap("PS5", 256, 512), ALU.mult)
+            mm(SWP, [(SWI, ap("U1"))], False, True)
 
-    def outa(c):
-        act(chunk("OUT", c), ZA, bias=ob, scale=om, off=lst("LOC", c))
+        def u1_g():
+            tt(ap("U1"), ap(cur), ap("PS5", 256, 512), ALU.mult)
+            mm(SWP, [(SWI, ap("U1"))], False, False)
 
-    def store(a, b):
-        o = ap("OUT", a * CH, b * CH)
-        stores.append(dma("s", T.yx[:, a * CH:b * CH], o[3], [o], []))
+        def go_g(p):
+            c0, c1, sc = part("C0", p), part("C1", p), part("SC", p)
+            ini = IN7 if p == 0 else col("SC", kb - 1)
+            ts(c0, far(p), TH, None, ALU.is_lt)
+            run("v", [c0, ini], [sc], lambda: g.vector.tensor_tensor_scan(sc[3], c0[3], c0[3], ini[3], ALU.add, ALU.max))
+            tt(c1, c0, part("FL", p), ALU.mult)
+            mm(ap(FB[p], 128, 128 + KP[p + 1] - KP[p]), [(W0, c0), (NBK, sc), (W1, c1), (NW0, c1)])
 
-    def small(y, i):
-        o = ap("FIN", 128 * i, 128 * i + 128)
-        stores.append(dma("s", y[:], o[3], [o], []))
+        def flag_g(p):
+            ts(part("XP", p), ap(FB[p], 128, 128 + KP[p + 1] - KP[p]), 0.0, None, ALU.is_gt)
+            mm(spart("PS3", p, 256), [(KI, part("XP", p))], False, False)
+            mm(cpart("PS3", p, 256), [(KI, part("XP", p))], False, p == 1)
 
-    outv(0)
-    outa(7)
-    store(0, 1)
-    store(7, 8)
-    outv(1)
-    outv(2)
-    act(ap("NHB"), NH)
-    mm(PAIR, [(PMB, ap("NHB"))])
-    watch(RO)
-    outa(8)
-    act(ap("XP"), PAIR, ACT.Abs, bias=-1.0)
-    watch2(float(-PAD))
-    outa(9)
-    store(1, 3)
-    store(8, 10)
-    tt(ap("U0", 0, 128), ss(cur), NH, ALU.mult)
-    flips(RO)
-    mm(ap("PS4", 256, 384), [(IB, FL)])
-    tt(ap("FIN", 128, 256), ap("TR", 0, 128), ap("TR", 128, 256), ALU.add)
-    tt(TL, ap("U0", 0, 128), ap("PS5", 128, 256), ALU.add)
-    tt(ap("U1", 0, 128), ap("TA"), ap("PS4", 256, 384), ALU.mult)
-    mm(ap("PS3", 256, 384), [(SWI, ap("U1", 0, 128))])
-    ts(ap("FIN", 0, 128), TL, float(-PAD), None, ALU.add)
-    outv(3)
-    tt(ap("FIN", 256, 384), ap("TA"), ap("PS3", 256, 384), ALU.add)
-    outa(10)
-    outa(11)
-    small(T.ytrig, 1)
-    small(T.ysrc, 0)
-    store(10, 12)
-    small(T.ytg, 2)
-    outv(4)
-    outa(12)
-    store(3, 5)
-    outv(5)
-    outa(13)
-    store(12, 14)
-    outv(6)
-    store(5, 7)
+        for p in range(2):
+            st["gG%d" % p] = lambda p=p: go_g(p)
+            st["fG%d" % p] = lambda p=p: flag_g(p)
+            st["tG%d" % p] = lambda p=p: ts(wide("SL", p, w0), wide("PS3", p, 256), -K, None, ALU.add)
+        def go_h(h):
+            c0, c1, sc = half("C0", h), half("C1", h), half("SC", h)
+            ini = IN7 if h == 0 else col("SC", 63)
+            ts(c0, half(FB[0], h), TH, None, ALU.is_lt)
+            run("v", [c0, ini], [sc], lambda: g.vector.tensor_tensor_scan(sc[3], c0[3], c0[3], ini[3], ALU.add, ALU.max))
+            tt(c1, c0, half("FL", h), ALU.mult)
+            mm(half("PS4", h), [(W0, c0), (NBK, sc), (W1, c1), (NW0, c1)])
+
+        def lists_h(h):
+            tt(half("TM", h, kb), half("SLOT", h, kb), half("PS4", h), ALU.min)
+            cp(half("SL", h, w0 + kb), half("TM", h, kb))
+
+        def lists_s():
+            tt(ap("TM", 0, 128), ap("SLOT", 0, 128), ap("PS4", 0, 128), ALU.min)
+            cp(ap("SL", w0, w0 + 128), ap("TM", 0, 128))
+
+        for h in range(2):
+            st["gH%d" % h] = lambda h=h: go_h(h)
+            st["tH%d" % h] = lambda h=h: lists_h(h)
+        st["tS"] = lists_s
+        st["locw"] = lambda: wrap(ap("PS6", 0, P // 16), BL, "LT", PAD, PAD + P) if t == 2 else None
+        st["locc"] = lambda: cp(ap("LOC", 0, P // 16), ap("PS6", 0, P // 16)) if t == 2 else None
+        st.update(amended(t))
+
+        def go_one():
+            ts(ap("C0"), far(0), TH, None, ALU.is_lt)
+            run("v", [ap("C0"), IN7], [ap("SC")], lambda: g.vector.tensor_tensor_scan(T.SC[:], T.C0[:], T.C0[:], IN7[3], ALU.add, ALU.max))
+            tt(ap("C1"), ap("C0"), FL, ALU.mult)
+            mm(ap(FB[0], 128, 256), [(W0, ap("C0")), (NBK, ap("SC")), (W1, ap("C1")), (NW0, ap("C1"))])
+
+        def list_one(a):
+            tt(ap("TM", a, a + 128), ap("SLOT", a, a + 128), ap(FB[0], 128, 256), ALU.min)
+            cp(ap("SL", w0 + a, w0 + a + 128), ap("TM", a, a + 128))
+
+        def locp(q):
+            a, n = (t - 1) * P // 2, P // 32
+            if q == "p":
+                wrap(ap("PS6", 0, n), BL, "LT", PAD + a, PAD + a + P // 2)
+            else:
+                cp(ap("LOC", a // 16, a // 16 + n), ap("PS6", 0, n))
+
+        def firsts2():
+            turned(ap("PS4", 0, 128), 0)
+            turned(ap("PS4", 128, 256), 256)
+            act(ap("SDO"), ap("PS4", 0, 256))
+            send(ap("SDI"), ap("SDO"), "asc")
+
+        st["g1"], st["ts"], st["tc"], st["f2"] = go_one, lambda: list_one(0), lambda: list_one(128), firsts2
+        st["lp"], st["lv"] = lambda: locp("p"), lambda: locp("v")
+        st["ps"] = lambda: pick("PS5", 0, "DG", 0, 2, 4)
+        st["pt"] = lambda: pick("PS5", 256, "MB", 0, 2, 4)
+        st["ea"] = lambda: act(ap("ET"), ap("PS5"))
+        st["pm"] = lambda: pick("PS3", 256, "LT", PAD + P, 2, 4)
+        st["em"] = lambda: act(ap("ET", 0, 256), ap("PS3", 256, 512))
+        st["lm"] = lambda: turned(ap("PS3", 0, 128), 0)
+        st["dd0"] = lambda: tt(ap("SDI", 128, 256), ap("SDI", 128, 256), ap("SDI", 0, 128), ALU.subtract, ext=[("asc", nin)])
+        st["u1G"] = u1_g
+        st["uA"], st["nhA"], st["u1A"] = kept_a, hits_a, u1_a
+        st["snA"] = lambda: mm(SWP, [(I32, ap(cur))], True, False)
+        st["slotA"] = lambda: act(ap("SLOT"), SWP)
+        st["watch"] = lambda: watch(t, 0.0)
+        st["dd"] = lambda: tt(ap("SDI", 128, 256), ap(TL[0], TL[1], TL[1] + 128), call(cur), ALU.subtract)
+        st["locm"] = lambda: wrap(ap("PS3", 0, 128), BL, "LT", PAD + P, YC)
+        for name in plan(t):
+            if ":" in name:
+                a, b = [128 * int(x) for x in name[2:].split(":")]
+                if name[0] == "w":
+                    st[name] = lambda q=name[1], a=a, b=b: look(q, a, b, int(a >= EP[1]))
+                else:
+                    st[name] = lambda q=name[1], a=a, b=b: turn(q, a, b)
+        for q in "av":
+            for c in range(4):
+                st["w%s%d" % (q, c)] = lambda q=q, c=c: look(q, c * CH, (c + 1) * CH, int(c * CH >= EP[1]))
+                st["i%s%d" % (q, c)] = lambda q=q, c=c: turn(q, c * CH, (c + 1) * CH)
+                st["y%s%d" % (q, c)] = lambda q=q, c=c: begin(q, c)
+            for h in range(2):
+                st["Y%s%d" % (q, h)] = lambda q=q, h=h: begin(q, h, M // 2)
+                st["o%s%d" % (q, h)] = lambda q=q, h=h: first(q, "DG", h, 0)
+                st["o%s%d" % (q, h + 2)] = lambda q=q, h=h: first(q, "MB", h, 128)
+                st["W%s%d" % (q, h)] = lambda q=q, h=h: look(q, EH[h], EH[h + 1], int(EH[h] >= EP[1]))
+                st["I%s%d" % (q, h)] = lambda q=q, h=h: turn(q, EH[h], EH[h + 1])
+        return st
+
+    def results():
+        cur = S[(RO - 1) % 2]
+        st = {}
+
+        def store(a, b):
+            o = span("X", OB[a], OB[b], PAD)
+            stores.append(dma("s", T.yx[:, OB[a]:OB[b]], o[3], [o], []))
+
+        def small(y, i):
+            o = ap("FIN", 128 * i, 128 * i + 128)
+            stores.append(dma("s", y[:], o[3], [o], []))
+
+        def hits():
+            act(ap("NHB"), NH)
+            mm(PAIR, [(PMB, ap("NHB"))])
+
+        def trigs():
+            watch(RO, float(-PAD))
+            tt(ap("FIN", 128, 256), ap("TR", 0, 128), ap("TR", 128, 256), ALU.add)
+            small(T.ytrig, 1)
+
+        def srcs():
+            for p in range(2):
+                tt(half("U0", p), shalf(cur, p), half("PS4", p), ALU.mult)
+            tt(ap("PS2", 0, 128), ap("U0", 0, 128), ap("PS5", 0, 128), ALU.add)
+            ts(ap("FIN", 0, 128), ap("PS2", 0, 128), float(-PAD), None, ALU.add)
+            small(T.ysrc, 0)
+
+        def swap():
+            flips(RO)
+            mm(ap("PS4", 256, 384), [(IB, FL)])
+            tt(ap("U1", 0, 128), TG, ap("PS4", 256, 384), ALU.mult)
+            mm(ap("PS3", 128, 256), [(SWI, ap("U1", 0, 128))])
+
+        def targets():
+            tt(ap("FIN", 256, 384), TG, ap("PS3", 128, 256), ALU.add)
+            small(T.ytg, 2)
+
+        OB = CFG["o"]
+        for c in range(len(OB) - 1):
+            a, b = OB[c], OB[c + 1]
+            st["ov%d" % c] = lambda a=a, b=b: ts(span("X", a, b, PAD), ZA, om, ob, ALU.mult, ALU.add, off=lspan("LOC", a, b))
+            st["oa%d" % c] = lambda a=a, b=b: act(span("X", a, b, PAD), ZA, bias=ob, scale=om, off=lspan("LOC", a, b))
+            for e in range(c + 1, len(OB)):
+                st["st%d_%d" % (c, e)] = lambda c=c, e=e: store(c, e)
+        for p in range(2):
+            st["nh%d" % p] = lambda p=p: wrap(half("PS4", p), BH, "I2", EH[p], EH[p + 1])
+            st["n%d" % p] = lambda p=p: wrap(half("PS5", p), BS, "I2", EH[p], EH[p + 1])
+        st.update(amended(RO))
+        st["nhb"], st["trigs"], st["srcs"], st["swap"], st["targets"] = hits, trigs, srcs, swap, targets
+        st["xp"] = lambda: act(ap("XP"), PAIR, ACT.Abs, bias=-1.0)
+        return st
+
+    for t in range(RO):
+        st, nxt = steps(t), steps(t + 1) if t < RO - 1 else results()
+        for name in plan(t):
+            if name.endswith("+"):
+                nxt[name[:-1]]()
+            else:
+                st[name]()
 
     for tok in stores:
         wait("s", tok)

from concourse.mybir import AluOpType, ActivationFunctionType

ALU = AluOpType
ACT = ActivationFunctionType
P, M, W, CAP, RO = 5120, 2048, 7168, 1024, 4
PAD = 128
YC = PAD + W
ZW = YC + M
K = 16384.0
CH = 512
CFG = {
    "x": [0, 2048, 4096, 6400, 7168],
    "kb": 64,
    "d": [0, 384, 1024, 1536, 2048],
    "s": [0, 512, 1024, 1536, 2048], "sl": [0, 512, 1024, 1536, 2048],
    "o": [0, 512, 1280, 2048, 2816, 3584, 4352, 5120, 5888, 6656, 7168],
    "first": "li ov3 cv2 t0 t1 t3 t2 b1 b0 b3 b2 fa0 fa1 go gate0 oa0 oa1 oa2 sw ya1 tw pre1 tm cv3 s1 s0 gate1 ya0 bands2 c1 c4 c2 pk ss s3 s2 "
             "D12 D01 c3 D34 D23 table firsts c5 c0 yv2 wa3 wa2 ya3 wv1 wv0 locm inv mg1 pre0 mg0 iv2 ia0 ia1 ia3 pre3 mg3 pre2 mg2 nh0+ tl0+",
    "round": "m0 n1 nh1 d0 tl1 m1 d1 n0 pre0 nhb n3 n2 m2 u0 xp fl Aa0 fa0 d2 m3 sn idx u1 go0 d3 gb0 a2 a3 fa1 pre1 slot tm0 s0 ss0 gb1 gb2 "
             "gb3 go1 s1 tm1 D01 s2 ss1 s3 Wa0 D12 D23 watch wa2 mg0 wv3 ia0 Ia1 pre2 iv1 mg1 mg2 pre3 D34 mg3 dd nh0+ tl0+",
    "last": "m1 n0 nh1 d1 n1 m0 nhb d0 m2 xp n2 n3 tl1 fl d2 u0 sn idx Aa0 m3 fa0 u1 go0 pre1 pre0 d3 slot tm0 ss0 a2 gb0 s0 D01 a3 gb1 gb3 gb2 "
            "fa1 go1 s1 tm1 D12 ss1 s3 s2 D24 Wa0 loc watch mg0 wv2 wa3 Ia1 Ia0 mg1 pre2 pre3 mg3 mg2 oa9+ oa1+ nh0+ nh1+ nhb+ oa7+ ov0+ ov2+ "
            "ov8+ ov4+ ov3+ st0_1+ st9_10+ st1_3+ st7_9+ st3_5+ oa5+ trigs+ n1+ n0+ xp+ oa6+ swap+ st5_7+ srcs+ targets+",
}

SCRATCH = {
    "X": ("sbuf", [128, YC], "bfloat16"), "Z": ("sbuf", [128, ZW], "bfloat16"), "LT": ("sbuf", [128, ZW], "bfloat16"),
    "LO": ("sbuf", [128, RO * M], "bfloat16"), "LAND": ("sbuf", [128, RO * M], "bfloat16"),
    "MB": ("sbuf", [128, M], "bfloat16"), "DB": ("sbuf", [128, M], "bfloat16"), "AB": ("sbuf", [128, M], "bfloat16"),
    "GB": ("sbuf", [128, M], "bfloat16"), "IW": ("sbuf", [128, 16 + M], "bfloat16"), "I2": ("sbuf", [128, M], "bfloat16"),
    "DG": ("sbuf", [128, M], "bfloat16"), "PK": ("sbuf", [128, W // 8], "bfloat16"),
    "D1": ("dram", [128, W // 8], "bfloat16"), "D2": ("dram", [128, W // 8], "bfloat16"),
    "LI": ("sbuf", [128, 384], "int32"), "THI": ("sbuf", [128, 8], "int32"),
    "TAO": ("sbuf", [128, 128], "uint16"), "TAU": ("sbuf", [128, 128], "uint16"),
    "STU": ("sbuf", [128, 256], "uint16"), "STI": ("sbuf", [128, 256], "uint16"), "SDO": ("sbuf", [128, 256], "float32"), "TLU": ("sbuf", [128, 128], "uint16"),
    "SL": ("sbuf", [128, RO * 256], "uint16"), "SSI": ("sbuf", [128, RO * 128], "uint16"), "SSW": ("sbuf", [128, RO * 256], "uint16"),
    "LOC": ("sbuf", [128, 448], "uint16"), "INV": ("sbuf", [128, 128], "uint16"), "IDX": ("sbuf", [128, 128], "uint16"),
    "SA": ("sbuf", [128, 256], "float32"), "SB": ("sbuf", [128, 256], "float32"),
    "SDI": ("sbuf", [128, 256], "float32"), "TR": ("sbuf", [128, 384], "float32"),
    "U0": ("sbuf", [128, 256], "float32"), "U1": ("sbuf", [128, 256], "float32"), "SLOT": ("sbuf", [128, 256], "float32"),
    "TM": ("sbuf", [128, 256], "float32"), "FIN": ("sbuf", [128, 384], "float32"),
    "NHB": ("sbuf", [128, 128], "bfloat16"), "XP": ("sbuf", [128, 128], "bfloat16"), "FL": ("sbuf", [128, 128], "bfloat16"),
    "C0": ("sbuf", [128, 128], "bfloat16"), "C1": ("sbuf", [128, 128], "bfloat16"), "SC": ("sbuf", [128, 128], "bfloat16"),
    "RI": ("sbuf", [128, 16], "int32"), "RJ": ("sbuf", [128, 16], "int32"), "RK": ("sbuf", [128, 8], "int32"),
    "RL": ("sbuf", [128, 16], "float32"), "CL": ("sbuf", [128, 16], "float32"), "HM": ("sbuf", [128, 80], "float32"),
    "RAMP": ("sbuf", [128, 128], "float32"), "KR": ("sbuf", [128, 128], "bfloat16"),
    "ONE": ("sbuf", [128, 128], "float32"), "W32": ("sbuf", [128, 3 * 128], "float32"),
    "FB": ("sbuf", [128, 144 + 4 * 128], "bfloat16"),
    "SEL": ("sbuf", [128, 32], "bfloat16"), "ET": ("sbuf", [128, 512], "bfloat16"), "NT": ("sbuf", [128, 128], "bfloat16"),
    "WB": ("sbuf", [128, 12 * 128], "bfloat16"), "BB": ("sbuf", [128, 5 * 144], "bfloat16"),
}
for _b in range(8):
    SCRATCH["PS%d" % _b] = ("psum", [128, 512], "float32")

NDMA = 24
SEMAPHORES = (["qv", "qa", "qp", "qg", "sent", "ata", "alt", "abk", "asc"] + ["d%d" % i for i in range(NDMA)]
              + ["as%d_%d" % (t, p) for t in range(RO) for p in range(2)] + ["al%d_%d" % (t, c) for t in range(RO) for c in range(5)])


def rank_program(g, core, T, topo):
    rank = T.rank_of(core)
    if rank is None:
        return
    dst = T.cores[(rank + 1) % len(T.cores)]
    src_core = T.cores[(rank - 1) % len(T.cores)]
    nin = len(topo.engines(src_core, core))
    nback = len(topo.engines(dst, core))
    odd = rank % 2

    Q = {"v": g.vector, "a": g.scalar, "p": g.tensor, "g": g, "s": g.sync}
    count = {"qv": 0, "qa": 0, "qp": 0, "qg": 0}
    known = {q: {} for q in Q}
    hist = {}
    clock = {}
    ndma = [0]
    sent = [0]
    stores = []

    def ap(name, a=0, b=None, step=1):
        t = T[name]
        if b is None:
            b = t.shape[1]
        return (name, a, b, t[:, a:b] if step == 1 else t[:, a:b:step])

    def col(name, j):
        return ap(name, j, j + 1)

    def wait(q, tok):
        if known[q].get(tok[0], 0) >= tok[1]:
            return
        Q[q].wait_ge(T.sem[tok[0]], tok[1])
        for s, v in clock.get(tok, {tok[0]: tok[1]}).items():
            if known[q].get(s, 0) < v:
                known[q][s] = v

    def order(q, reads, writes, ext):
        need = {}
        for regs, w in ((reads, False), (writes, True)):
            for (name, a, b, _) in regs:
                ps = name.startswith("PS")
                for (a2, b2, w2, q2, tok) in hist.get(name, []):
                    if ps:
                        hit = q2 != q or (q != "p" and (w or w2) and a < b2 and a2 < b)
                    else:
                        hit = (w or w2) and a < b2 and a2 < b
                    if hit and need.get(tok[0], 0) < tok[1]:
                        need[tok[0]] = tok[1]
        for tok in list(ext) + sorted(need.items()):
            wait(q, tuple(tok))

    def note(q, reads, writes, tok):
        c = dict(known[q])
        c[tok[0]] = tok[1]
        clock[tok] = c
        for regs, w in ((reads, False), (writes, True)):
            for (name, a, b, _) in regs:
                h = hist.setdefault(name, [])
                if w:
                    h[:] = [e for e in h if not (a <= e[0] and e[1] <= b)]
                h.append((a, b, w, q, tok))

    def run(q, reads, writes, fn, ext=()):
        order(q, reads, writes, ext)
        s = "q" + q
        count[s] += 1
        fn().then_inc(T.sem[s], 1)
        note(q, reads, writes, (s, count[s]))

    def dma(q, out, in_, reads, writes, ext=()):
        order(q, reads, writes, ext)
        s = "d%d" % ndma[0]
        ndma[0] += 1
        Q[q].dma_start(out, in_).then_inc(T.sem[s], 16)
        note(q, reads, writes, (s, 16))
        return (s, 16)

    def send(land, src, sem, to=dst):
        order("g", [src], [], ())
        rid, pid, _ = topo.addr(to)
        g.remote_dma(land[3], src[3], T.sem[sem], T.sem.sent, pid, rid, topo.mask(core, to))
        sent[0] += len(topo.engines(core, to))

    def aps(*xs):
        return [x for x in xs if isinstance(x, tuple)]

    def raw(x):
        return x[3] if isinstance(x, tuple) else x

    def ind(win, off):
        return win[3].indirect(off[3])

    def ts(out, in0, s1, s2, op0, op1=None, off=None, ext=()):
        i0 = in0[3] if off is None else ind(in0, off)
        if op1 is None:
            run("v", aps(in0, s1, off), [out], lambda: g.vector.tensor_scalar(out[3], i0, raw(s1), None, op0), ext)
        else:
            run("v", aps(in0, s1, s2, off), [out], lambda: g.vector.tensor_scalar(out[3], i0, raw(s1), raw(s2), op0, op1), ext)

    def tt(out, in0, in1, op, off=None, ext=()):
        i0 = in0[3] if off is None else ind(in0, off)
        run("v", aps(in0, in1, off), [out], lambda: g.vector.tensor_tensor(out[3], i0, in1[3], op), ext)

    def cp(out, in_, off=None, ext=()):
        i0 = in_[3] if off is None else ind(in_, off)
        run("v", aps(in_, off), [out], lambda: g.vector.tensor_copy(out[3], i0), ext)

    def fill(out, value):
        run("v", [], [out], lambda: g.vector.memset(out[3], value))

    def act(out, in_, func=ACT.Identity, bias=0.0, scale=1.0, off=None, ext=()):
        i0 = in_[3] if off is None else ind(in_, off)
        run("a", aps(in_, bias, scale, off), [out],
            lambda: g.scalar.activation(out[3], i0, func, bias=raw(bias), scale=raw(scale)), ext)

    def gather(q, out, win, off, ext=()):
        if q == "v":
            cp(out, win, off, ext)
        else:
            act(out, win, off=off, ext=ext)

    def mm(out, pairs, start=True, stop=True, ext=()):
        def fn():
            for i, (l, r) in enumerate(pairs):
                ins = g.tensor.matmul(out[3], l[3], r[3], start and i == 0, stop and i == len(pairs) - 1)
            return ins
        run("p", [x for pr in pairs for x in pr], [out], fn, ext)

    def iota(out, pattern, base, cm, flt=True):
        if flt:
            run("g", [], [out], lambda: g.iota(out[3], pattern, base, cm, allow_small_or_imprecise_dtypes=True))
        else:
            run("g", [], [out], lambda: g.iota(out[3], pattern, base, cm))

    def sel(out, in_, pattern, cmp, value, base, cm):
        run("g", [in_], [out], lambda: g.affine_select(out[3], in_[3], pattern, cmp, value, base, cm))

    def chunk(name, c, base=0, n=CH):
        return ap(name, base + c * n, base + (c + 1) * n)

    def lst(name, c, base=0, n=CH):
        return ap(name, base + c * n // 16, base + (c + 1) * n // 16)

    def span(name, a, b, base=0):
        return ap(name, base + a, base + b)

    def lspan(name, a, b, base=0):
        return ap(name, base + a // 16, base + b // 16)

    BF, BH, BL, BS, BN = 0, 1, 2, 3, 4

    def wrap(out, kind, name, a, b, start=True, stop=True):
        mm(out, [(ap("BB", kind * 144 + 15 - r, kind * 144 + 143 - r), ap(name, a + r, b, 16)) for r in range(16)], start, stop)

    def pick(bank, base, name, a, d0, d1):
        end, cols = base + 128 * (d1 - d0), ap("SEL", 8 * d0, 8 * d1)

        def fn():
            for r in range(16):
                ins = g.tensor.matmul(T[bank][:, base + r:end:16], T[name][:, a + r:a + M:16], cols[3], True, True)
            return ins
        run("p", [ap(name, a, a + M), cols], [ap(bank, base, end)], fn)

    def turned(out, a, more=(), start=True, stop=True):
        mm(out, [(ap("ET", a, a + 128), I128), (ap("ET", a + 128, a + 256), IB)] + list(more), start, stop)

    def band(kind, scale):
        act(ap("BB", kind * 144, kind * 144 + 144), ap("BB", 0, 144), scale=scale)

    I32, PM32, SWI = [ap("W32", i * 128, (i + 1) * 128) for i in range(3)]
    IB, N16, DSG, PMB, NBK, W0, W1, NW0, KI, NKI, BK, I128 = [ap("WB", i * 128, (i + 1) * 128) for i in range(12)]
    ONES, ONEB = ap("FB", 0, 144), ap("FB", 0, 128)
    FK, FNK, F16, FSG = [ap("FB", 144 + i * 128, 272 + i * 128) for i in range(4)]
    WS, WL, IC, SG, IN7, TH, PH, PL, PB = [col("CL", j) for j in range(9)]
    R4, HC, LC = col("RL", 4), col("RL", 2), col("RL", 10)
    XX, ZX, ZA, LTX = ap("X"), ap("Z", 0, YC), ap("Z"), ap("LT", 0, YC)
    XB, DBN, kb = CFG["x"], CFG["d"], CFG["kb"]
    KP = [0, kb, 128]
    EP = [0, 16 * kb, M]
    HP, EH = [0, 64, 128], [0, M // 2, M]

    def half(name, h, base=0):
        return ap(name, base + HP[h], base + HP[h + 1])

    def shalf(name, h, base=0):
        return half(name, h, base + (128 * h if kb == 64 else 0))

    def part(name, p, base=0):
        return ap(name, base + KP[p], base + KP[p + 1])

    def wide(name, p, base=0):
        return ap(name, base + 2 * KP[p], base + 2 * KP[p + 1])

    def cpart(name, p, base=0):
        return part(name, p, base + kb)

    def spart(name, p, base=0):
        return part(name, p, base + 128 * p)

    def call(name, base=0):
        return ap(name, base + kb, base + kb + 128)

    def twice(name, base, mat, src):
        for p in range(2):
            if KP[p] < KP[p + 1]:
                mm(spart(name, p, base), [(mat, part(src, p))])
        mm(call(name, base), [(mat, ap(src))])

    TG, SRC, TRG = ap("LI", 0, 128), ap("LI", 128, 256), ap("LI", 256, 384)
    dma("s", TG[3], T.tg[:], [], [TG])
    dma("s", SRC[3], T.src[:], [], [SRC])
    dma("s", TRG[3], T.trig[:], [], [TRG])
    for c in range(len(XB) - 1):
        z = span("X", XB[c], XB[c + 1], PAD)
        dma("s", z[3], T.x[:, XB[c]:XB[c + 1]], [], [z])
    dma("s", col("THI", 0)[3], T.th[:], [], [col("THI", 0)])

    iota(ap("RI"), [[-1, 16]], 16, 1, False)
    iota(ap("RAMP"), [[1, 128]], 0, 0)
    fill(ONES, 1.0)
    fill(ap("X", 0, PAD), 0.0)
    fill(ap("C1", 0, 64), -16.0 if odd else -1.0)
    bf = ap("BB", 0, 144)
    sel(bf, ONES, [[0, 9], [1, 16]], ALU.is_equal, 0.0, -15, 0)
    sel(bf, bf, [[-16, 9], [0, 16]], ALU.is_ge, 0.0, 0, 1)
    sel(bf, bf, [[16, 9], [0, 16]], ALU.is_ge, 0.0, 15, -1)
    sel(IB, ONEB, [[-1, 128]], ALU.is_equal, 0.0, 0, 1)
    ts(ap("RJ"), ap("RI"), 15, None, ALU.bitwise_and)
    fill(ap("Z", 0, PAD), 0.0)
    ts(ap("RL"), ap("RJ"), 0.0, None, ALU.is_equal)
    cp(IC, col("RJ", 0))
    act(PH, IC, ACT.Sign, bias=7.5, scale=-1.0)
    act(PL, PH, bias=0.5, scale=-0.5)
    act(PH, PH, bias=0.5, scale=0.5)
    act(PB, IC, bias=1.0, scale=7.0)
    act(PB, PB, scale=PH)
    act(ap("CL", 9, 12), ap("RAMP", 1, 4), scale=PH)
    act(col("CL", 11), PH, scale=4.0)
    act(ap("PK", 0, 128), ap("RAMP"), bias=PB, scale=PL)
    act(WL, HC, bias=LC, scale=128.0)
    act(IN7, col("RL", 0), scale=7.0)
    band(BL, WL)
    act(ap("BB", BN * 144, BN * 144 + 144), ap("BB", BL * 144, BL * 144 + 144), scale=-1.0)
    HY = YC // 128
    ts(ap("HM", 0, 16), ap("RAMP", 0, 16), HC, None, ALU.mult)
    ts(ap("HM", 16, 80), ap("RAMP", 0, 64), float(-HY), HC, ALU.add, ALU.mult)
    ts(col("CL", 15), HC, float(HY), None, ALU.mult)
    ts(ap("LT", YC, YC + 128), ap("RAMP"), LC, col("CL", 15), ALU.mult, ALU.add)
    n = 128
    while n < M:
        ts(ap("LT", YC + n, YC + 2 * n), ap("LT", YC, YC + n), col("HM", n // 128), None, ALU.add)
        n *= 2
    act(ap("LT", 0, M), ap("LT", YC, ZW), bias=col("HM", 16))
    ts(ap("LT", 3 * M, YC), ap("LT", YC, YC + YC - 3 * M), col("HM", 64), None, ALU.add)
    ts(ap("TAO"), TG, float(PAD), None, ALU.add)
    send(ap("TAU"), ap("TAO"), "ata")
    ATA = [("ata", nin)]
    ts(ap("LT", 2 * M, 3 * M), ap("LT", YC, ZW), col("HM", 48), None, ALU.add)
    ts(ap("STU"), ap("LI", 128, 384), float(PAD), None, ALU.add)
    send(ap("STI"), ap("STU"), "abk", src_core)
    ts(ap("LT", M, 2 * M), ap("LT", YC, ZW), col("HM", 32), None, ALU.add)
    act(col("LT", 0), R4)
    run("v", [ap("LT", YC, ZW), ap("TAO")], [LTX], lambda: g.vector.tensor_copy(ind(LTX, ap("TAO")), T.LT[:, YC:ZW]))
    rows = [T.LT[j:128:8, PAD:YC] for j in (0, 2)]
    LTR = ap("LT", PAD, YC)
    dma("s", T.D1[:], rows[1], [LTR], [ap("D1")])

    def blocks(out, in_, n):
        sel(out, in_, [[-n, 128 // n], [0, n]], ALU.is_ge, 0.0, 0, 1)
        sel(out, out, [[n, 128 // n], [0, n]], ALU.is_ge, 0.0, n - 1, -1)

    def diag(out, in_):
        sel(out, in_, [[-1, 128]], ALU.is_equal, 0.0, 0, 1)

    def later(out, in_, pattern, base, value):
        sel(out, in_, pattern, ALU.is_ge, 0.0, base, 1)
        sel(out, out, pattern, ALU.not_equal, value, base, 1)

    iota(FK, [[0, 128]], int(K), 0)
    blocks(BK, FK, 16)
    later(W0, BK, [[-1, 128]], 0, K * (CAP + 8))
    iota(FNK, [[0, 128]], int(-K), 0)
    blocks(NBK, FNK, 16)
    iota(F16, [[0, 128]], -16, 0)
    diag(N16, F16)

    def exchange():
        sel(SWI, ap("ONE"), [[-2, 64], [1, 2]], ALU.is_equal, 0.0, -1, 1)
        sel(SWI, SWI, [[-1, 128]], ALU.not_equal, -1.0, 0, 1)

    later_ones = {
        "c6": lambda: (sel(ap("SEL"), ap("FB", 0, 32), [[-2, 2], [-8, 2], [-16, 8]], ALU.is_equal, 0.0, 0, 1),
                       iota(I128, [[0, 128]], 128, 0), diag(I128, I128)),
        "c0": lambda: (blocks(PMB, ONEB, 2), diag(KI, FK)),
        "c1": lambda: (iota(FSG, [[0, 64], [-2, 2]], 1, 0), diag(DSG, FSG), iota(ap("KR"), [[-1, 128]], 0, 0)),
        "c2": lambda: (iota(ap("ONE"), [[0, 128]], 1, 0), exchange()),
        "c3": lambda: later(W1, BK, [[-2, 64], [1, 2]], -1, K * (CAP + 8)),
        "c4": lambda: later(NW0, NBK, [[-1, 128]], 0, -K * (CAP + 8)),
        "c5": lambda: (diag(I32, ap("ONE")), diag(NKI, FNK)),
    }

    cm, cb = (-1.0, 16.0) if odd else (1.0, 1.0)
    om, ob = (-1.0, 16.0) if odd else (1.0, -1.0)

    def conv(q, c):
        x, z = span("X", XB[c], XB[c + 1], PAD), span("Z", XB[c], XB[c + 1], PAD)
        if q == "v":
            ts(z, x, cm, cb, ALU.mult, ALU.add)
        else:
            act(z, x, bias=cb, scale=cm)

    S = ["SA", "SB"]
    T1P, TL = ("PS2", 0), ("PS2", 128)
    n = 128
    while n < W // 8:
        m = min(n, W // 8 - n)
        act(ap("PK", n, n + m), ap("PK", 0, m), bias=col("CL", 9 + n // 256))
        n *= 2
    conv("a", 0)
    conv("a", 1)

    FB = ["PS6", "PS7"]
    NH = ap("PS4", 0, 128)
    PAIR, IXP, SWP = ap("PS3", 0, 128), ap("PS3", 128, 256), ap("PS3", 256, 512)
    QB = ["PS0", "PS1"] + (["PS7"] if kb == 128 else [])
    nq = len(QB)
    TB = [ap("PS0"), ap("PS1"), ap("PS3"), ap("PS5")]
    FL = ap("FL")
    gs, gb = (-16.0, 144.0) if odd else (16.0, -128.0)

    def far(p):
        return ap(FB[p], 0, KP[p + 1] - KP[p])

    def farh(h):
        return far(h) if kb == 64 else half(FB[0], h)

    def flips(t):
        if t == 1:
            ts(FL, ap("XP"), 0.0, None, ALU.is_equal)
        else:
            tt(FL, FL, ap("XP"), ALU.is_equal)

    def watch(t, shift):
        both = [(I32, ap("TR", 0, 128)), (I32, ap("TR", 128, 256))] if t > 1 else [(I32, ap("TR", 256, 384))]
        mm(ap("PS3", 256, 384), both + [(KI, ap("NHB"))])
        for h in range(2):
            mm(half("PS3", h, 384), [(I32, shalf(S[(t + 1) % 2], h) if t > 1 else half("TR", h, 128)), (NKI, half("NHB", h))])
        act(ap("TR", 0, 128), ap("PS3", 256, 384), ACT.Relu, bias=shift - K)
        act(ap("TR", 128, 256), ap("PS3", 384, 512), ACT.Relu, bias=shift)

    def amended(t):
        st = {}

        def hits():
            act(ap("NHB"), NH)
            mm(PAIR, [(PMB, ap("NHB"))])

        def kn():
            for a in (256, 384):
                mm(ap("PS4", a, a + 128), [(ap("NT"), KI)])

        st["x1"] = lambda: pick("PS6", 0, "I2", 0, 0, 4)
        st["xv"] = lambda: ts(ap("NT"), ap("PS6", 256, 384), 0.0, None, ALU.is_equal)
        st["xa"] = lambda: act(ap("NT"), ap("PS6", 256, 384), ACT.Relu, bias=1.0, scale=-1.0)
        st["x2"] = lambda: mm(NH, [(ap("NT"), IB)])
        st["Ea"] = lambda: act(ap("ET"), ap("PS6"))
        st["Ev"] = lambda: cp(ap("ET"), ap("PS6"))
        st["Es"] = lambda: act(ap("ET", 0, 256), ap("PS6", 0, 256))
        st["x3"] = lambda: turned(ap("PS5", 0, 128), 0)
        st["x4"] = lambda: turned(ap("PS5", 128, 256), 256)
        st["hb"], st["kn"] = hits, kn
        return st

    def plan(t):
        return CFG["first" if t == 0 else "last" if t == RO - 1 else "round"].split()

    def steps(t):
        cur, old = S[t % 2], S[(t + 1) % 2]
        win = ZX if t == 0 else ZA
        w0, l0 = t * 256, t * 128
        SB = CFG["sl" if t == RO - 1 else "s"]
        st = {}

        def dist0(c):
            act(chunk("DB", c), XX, scale=-1.0, off=lst("STU", c, 128))
            mm(TB[c], [(IB, chunk("X", c, PAD + P)), (IB, chunk("DB", c))])

        def dist(c):
            a, b = DBN[c], DBN[c + 1]
            act(span("DB", a, b), ZA, scale=-1.0, off=lspan("TLU", a, b))
            mm(ap(QB[c % 2], 0, b - a), [(IB, span("MB", a, b)), (IB, span("DB", a, b))])

        def begin(q, c, n=CH):
            if q == "v":
                ts(chunk("Z", c, YC, n), XX, cm, cb, ALU.mult, ALU.add, off=lst("TAU", c, 0, n), ext=ATA)
            else:
                act(chunk("Z", c, YC, n), XX, bias=cb, scale=cm, off=lst("TAU", c, 0, n), ext=ATA)

        def gate(h):
            ts(span("GB", EH[h], EH[h + 1]), span("X", EH[h], EH[h + 1], PAD + P), 7.5, 16.0, ALU.is_gt, ALU.mult)

        def size(q, a, b):
            zero = 0.0 if t else cb
            if q == "v":
                ts(span("AB", a, b), span("DB", a, b), zero, -2.0, ALU.min, ALU.mult)
            else:
                act(span("AB", a, b), span("DB", a, b), ACT.Abs, bias=-zero)

        begun = [False, False]

        def total(h, name):
            o = farh(h) if t else half(FB[0], h)
            wrap(o, BF, name, EH[h], EH[h + 1], not begun[h], name == "AB")
            if name == "DB" and t == 0:
                mm(o, [(N16, ap("C1", 0, 64))], False, False)
            begun[h] = True

        def numbering():
            cp(TH, col("THI", 0))
            ts(ap("TR", 128, 384), ap("LI", 128, 384), float(PAD), None, ALU.add)

        def go0():
            ts(ap("C0"), ap(FB[0], 0, 128), TH, None, ALU.is_lt)
            run("v", [ap("C0"), IN7], [ap("SC")], lambda: g.vector.tensor_tensor_scan(T.SC[:], T.C0[:], T.C0[:], IN7[3], ALU.add, ALU.max))
            mm(ap(FB[0], 128, 256), [(W0, ap("C0")), (NBK, ap("SC"))])

        def lists0():
            tt(ap("TM", 0, 128), ap("TR", 128, 256), ap(FB[0], 128, 256), ALU.min)
            cp(ap("SL", 0, 128), ap("TM", 0, 128))

        def kept():
            if t > 1:
                tt(ap("U0"), ap(old), ap("PS4", 256, 512), ALU.min)
                return
            for h in range(2):
                tt(shalf("U0", h), half("TR", h, 128), shalf("PS4", h, 256), ALU.min)
            tt(call("U0"), ap("SDI", 0, 128), call("PS4", 256), ALU.min, ext=[("asc", nin)])

        def table():
            dma("s", rows[0], T.PK[:], [ap("PK")], [LTR])
            mine = hist["LT"].pop()
            dma("s", rows[1], T.D2[:], [], [LTR], [("alt", nin)])
            hist["LT"].append(mine)

        def go(p):
            c0, c1, sc = part("C0", p), part("C1", p), part("SC", p)
            ini = IN7 if p == 0 else col("SC", kb - 1)
            ts(c0, far(p), TH, None, ALU.is_lt)
            run("v", [c0, ini], [sc], lambda: g.vector.tensor_tensor_scan(sc[3], c0[3], c0[3], ini[3], ALU.add, ALU.max))
            n = KP[p + 1] - KP[p]
            tt(c1, c0, part("FL", p), ALU.mult)
            for j in range(2):
                mm(ap(FB[p], 128 + j * n, 128 + (j + 1) * n), [(W0, c0), (NBK, sc), (W1, c1), (NW0, c1)])

        def lists(p):
            n = KP[p + 1] - KP[p]
            tt(wide("TM", p), wide("SLOT", p), ap(FB[p], 128, 128 + 2 * n), ALU.min)
            cp(wide("SL", p, w0), wide("TM", p))

        def numbers(c):
            a, b = SB[c], SB[c + 1]
            tt(span("LO", a, b, t * M), win, span("GB", a, b), ALU.min, off=lspan("SL", a, b, w0 + kb if t else 0))

        def numbers_a(c):
            a, b = SB[c], SB[c + 1]
            act(span("DB", a, b), win, scale=-1.0, off=lspan("SL", a, b, w0 + kb))
            mm(ap("PS4", 0, b - a), [(IB, span("DB", a, b)), (IB, span("GB", a, b))])

        def out(a, b):
            send(span("LAND", SB[a], SB[b], t * M), span("LO", SB[a], SB[b], t * M), "al%d_%d" % (t, a))

        piece = {}
        for name in plan(t):
            if name[0] == "D":
                a, b = int(name[1]), int(name[2])
                st[name] = lambda a=a, b=b: out(a, b)
                piece.update({c: a for c in range(a, b)})

        def look(q, a, b, p):
            if "ssW" in plan(t):
                gather(q, span("IW", a, b, 16), LTX, lspan("SSW", a, b, w0 + 128 * p), [("as%d_0" % t, nin)])
            elif a < b:
                gather(q, span("IW", a, b, 16), LTX, lspan("SSI", a, b, l0), [("as%d_%d" % (t, p if t else 0), nin)])

        def turn(q, a, b):
            if a < b:
                gather(q, span("I2", a, b), ap("IW"), lspan("INV", a, b))

        def merge(c):
            al = [("al%d_%d" % (t, piece[c]), nin)]
            a, b = SB[c], SB[c + 1]
            mm(ap(QB[c % nq], 0, b - a), [(N16, span("LAND", a, b, t * M))], False, True, ext=al)
            tt(span("Z", a, b, YC), span("LAND", a, b, t * M), ap(QB[c % nq], 0, b - a), ALU.max, ext=al)

        def trig(a, b, s):
            tt(span("PS2", a, b), span("SDI", a, b, 128), span("PS4", a, b), ALU.mult, ext=[("asc", nin)])
            tt(span("PS2", a, b, 128), span("PS2", a, b), span("SDI", a, b) if t == 1 else span(s, a, b, kb), ALU.add)
            cp(span("TLU", a, b), span("PS2", a, b, 128))

        def nhb():
            act(ap("NHB"), NH)
            mm(PAIR, [(PMB, ap("NHB"))])
            twice("PS4", 256, KI, "NHB")

        def fl():
            flips(t)
            mm(IXP, [(N16, ap("KR")), (DSG, FL)])
            twice("PS5", 256, IB, "FL")

        def u1():
            tt(ap("U1"), ap(cur), ap("PS5", 256, 512), ALU.mult)
            mm(SWP, [(SWI, ap("U1"))])

        def loc():
            wrap(ap("PS6", 0, P // 16), BL, "LT", PAD, PAD + P)
            cp(ap("LOC", 0, P // 16), ap("PS6", 0, P // 16))

        def first(q, name, h, base):
            gather(q, span(name, EH[h], EH[h + 1]), LTX, half("STI", h, base), [("abk", nback)])

        def firsts():
            act(ap("SDO"), ap("PS4", 0, 256))
            send(ap("SDI"), ap("SDO"), "asc")

        def wraps():
            wrap(ap("PS4", 0, 128), BL, "DG", 0, M)
            wrap(ap("PS4", 128, 256), BN, "DG", 0, M, True, False)

        def inv():
            cp(ap("LOC", P // 16, 448), ap("PS3", 0, 128))
            ts(ap("INV"), ap("PS3", 0, 128), float(16 - YC), None, ALU.add)

        def bands2():
            act(WS, col("RL", 0), bias=col("RL", 8), scale=128.0)
            band(BH, R4)
            band(BS, WS)
            act(ap("IW", 0, 16), ap("Z", 0, 16), bias=R4)

        st["bands2"] = bands2
        st.update(later_ones)

        for c in range(4):
            st["t%d" % c] = lambda c=c: dist0(c)
            st["b%d" % c] = lambda c=c: act(chunk("AB", c), TB[c], ACT.Abs)
            st["v%d" % c] = lambda c=c: tt(chunk("DB", c), ZX, chunk("X", c, PAD + P), ALU.add if odd else ALU.subtract, off=lst("STU", c, 128))
            st["bv%d" % c] = lambda c=c: size("v", c * CH, (c + 1) * CH)
            st["ba%d" % c] = lambda c=c: size("a", c * CH, (c + 1) * CH)
            st["cv%d" % c] = lambda c=c: conv("v", c)
            st["ca%d" % c] = lambda c=c: conv("a", c)
            st["gb%d" % c] = lambda c=c: act(chunk("GB", c), ap("MB"), ACT.Relu, bias=gb, scale=gs, off=lst("IDX", c))
        for c in range(len(SB) - 1):
            st["s%d" % c] = lambda c=c: numbers(c)
            st["g%d" % c] = lambda c=c: act(span("GB", SB[c], SB[c + 1]), ap("MB"), ACT.Relu, bias=gb, scale=gs, off=lspan("IDX", SB[c], SB[c + 1]))
            st["gc%d" % c] = lambda c=c: act(span("GB", SB[c], SB[c + 1]), ap("MB"), ACT.Relu, bias=16.0 - gb, scale=-gs,
                                             off=lspan("IDX", SB[c], SB[c + 1]))
            st["sa%d" % c] = lambda c=c: numbers_a(c)
            st["sb%d" % c] = lambda c=c: act(span("LO", SB[c], SB[c + 1], t * M), ap("PS4", 0, SB[c + 1] - SB[c]), ACT.Relu, scale=-1.0)
            st["pre%d" % c] = lambda c=c: mm(ap(QB[c % nq], 0, SB[c + 1] - SB[c]), [(IB, span("Z", SB[c], SB[c + 1], YC))], True, False)
            st["mg%d" % c] = lambda c=c: merge(c)
        for c in range(len(DBN) - 1):
            st["m%d" % c] = lambda c=c: gather("a", span("MB", DBN[c], DBN[c + 1]), ZA, lspan("LOC", DBN[c], DBN[c + 1], P // 16))
            st["d%d" % c] = lambda c=c: tt(span("DB", DBN[c], DBN[c + 1]), win, span("MB", DBN[c], DBN[c + 1]), ALU.subtract,
                                           off=lspan("TLU", DBN[c], DBN[c + 1]))
            st["a%d" % c] = lambda c=c: size("a", DBN[c], DBN[c + 1])
            st["av%d" % c] = lambda c=c: size("v", DBN[c], DBN[c + 1])
            st["e%d" % c] = lambda c=c: dist(c)
            st["f%d" % c] = lambda c=c: act(span("AB", DBN[c], DBN[c + 1]), ap(QB[c % 2], 0, DBN[c + 1] - DBN[c]), ACT.Abs)
        for p in range(2):
            st["Av%d" % p] = lambda p=p: size("v", EH[p], EH[p + 1])
            st["Aa%d" % p] = lambda p=p: size("a", EH[p], EH[p + 1])
            st["GB%d" % p] = lambda p=p: act(span("GB", EH[p], EH[p + 1]), ap("MB"), ACT.Relu, bias=gb, scale=gs, off=half("IDX", p))
            st["fd%d" % p] = lambda p=p: total(p, "DB")
            st["fa%d" % p] = lambda p=p: total(p, "AB")
            st["gate%d" % p] = lambda p=p: gate(p)
            st["go%d" % p] = lambda p=p: go(p)
            st["tm%d" % p] = lambda p=p: lists(p)
            st["ss%d" % p] = lambda p=p: send(part("SSI", p, l0), spart("SL", p, w0), "as%d_%d" % (t, p))
            st["nh%d" % p] = lambda p=p: wrap(half("PS4", p), BH, "I2", EH[p], EH[p + 1])
            st["n%d" % p] = lambda p=p: wrap(half("PS5", p, kb), BL, "I2", EH[p], EH[p + 1])
            st["n%d" % (p + 2)] = lambda p=p: wrap(shalf("PS5", p), BS, "I2", EH[p], EH[p + 1])
            st["tl%d" % p] = lambda p=p: trig(HP[p], HP[p + 1], old)
        st["tl"] = lambda: trig(0, 128, old)
        st["li"], st["table"], st["go"], st["tm"], st["u0"] = numbering, table, go0, lists0, kept
        st["ss"] = lambda: send(ap("SSI", 0, 128), ap("SL", 0, 128), "as0_0")
        st["ssW"] = lambda: send(ap("SSW", w0, w0 + 256), ap("SL", w0, w0 + 256), "as%d_0" % t)
        st["pk"] = lambda: send(ap("D2"), ap("D1"), "alt")
        st["nhb"], st["fl"], st["u1"], st["loc"], st["inv"] = nhb, fl, u1, loc, inv
        st["sw"], st["firsts"] = wraps, firsts
        st["tw"] = lambda: wrap(ap("PS4", 128, 256), BL, "MB", 0, M, False, True)
        st["xp"] = lambda: act(ap("XP"), PAIR, ACT.Abs, bias=-1.0)
        st["idx"] = lambda: ts(ap("IDX"), IXP, IC, None, ALU.add)
        st["sn"] = lambda: tt(ap(cur), ap("U0"), ap("PS5", 0, 256), ALU.add)
        st["slot"] = lambda: tt(ap("SLOT"), ap(cur), SWP, ALU.add)
        def kept_a():
            for h in range(2):
                mm(shalf("PS4", h, 256), [(I32, shalf(old, h) if t > 1 else half("TR", h, 128)), (KI, half("NHB", h))])
            mm(call("PS4", 256), [(I32, call(old) if t > 1 else ap("SDI", 0, 128)), (KI, ap("NHB"))], ext=[("asc", nin)])
            act(ap("U0"), ap("PS4", 256, 512), ACT.Relu, bias=-K)

        def hits_a():
            act(ap("NHB"), NH)
            mm(PAIR, [(PMB, ap("NHB"))])

        def u1_a():
            tt(ap("U1"), ap(cur), ap("PS5", 256, 512), ALU.mult)
            mm(SWP, [(SWI, ap("U1"))], False, True)

        def u1_g():
            tt(ap("U1"), ap(cur), ap("PS5", 256, 512), ALU.mult)
            mm(SWP, [(SWI, ap("U1"))], False, False)

        def go_g(p):
            c0, c1, sc = part("C0", p), part("C1", p), part("SC", p)
            ini = IN7 if p == 0 else col("SC", kb - 1)
            ts(c0, far(p), TH, None, ALU.is_lt)
            run("v", [c0, ini], [sc], lambda: g.vector.tensor_tensor_scan(sc[3], c0[3], c0[3], ini[3], ALU.add, ALU.max))
            tt(c1, c0, part("FL", p), ALU.mult)
            mm(ap(FB[p], 128, 128 + KP[p + 1] - KP[p]), [(W0, c0), (NBK, sc), (W1, c1), (NW0, c1)])

        def flag_g(p):
            ts(part("XP", p), ap(FB[p], 128, 128 + KP[p + 1] - KP[p]), 0.0, None, ALU.is_gt)
            mm(spart("PS3", p, 256), [(KI, part("XP", p))], False, False)
            mm(cpart("PS3", p, 256), [(KI, part("XP", p))], False, p == 1)

        for p in range(2):
            st["gG%d" % p] = lambda p=p: go_g(p)
            st["fG%d" % p] = lambda p=p: flag_g(p)
            st["tG%d" % p] = lambda p=p: ts(wide("SL", p, w0), wide("PS3", p, 256), -K, None, ALU.add)
        def go_h(h):
            c0, c1, sc = half("C0", h), half("C1", h), half("SC", h)
            ini = IN7 if h == 0 else col("SC", 63)
            ts(c0, half(FB[0], h), TH, None, ALU.is_lt)
            run("v", [c0, ini], [sc], lambda: g.vector.tensor_tensor_scan(sc[3], c0[3], c0[3], ini[3], ALU.add, ALU.max))
            tt(c1, c0, half("FL", h), ALU.mult)
            mm(half("PS4", h), [(W0, c0), (NBK, sc), (W1, c1), (NW0, c1)])

        def lists_h(h):
            tt(half("TM", h, kb), half("SLOT", h, kb), half("PS4", h), ALU.min)
            cp(half("SL", h, w0 + kb), half("TM", h, kb))

        def lists_s():
            tt(ap("TM", 0, 128), ap("SLOT", 0, 128), ap("PS4", 0, 128), ALU.min)
            cp(ap("SL", w0, w0 + 128), ap("TM", 0, 128))

        for h in range(2):
            st["gH%d" % h] = lambda h=h: go_h(h)
            st["tH%d" % h] = lambda h=h: lists_h(h)
        st["tS"] = lists_s
        st["locw"] = lambda: wrap(ap("PS6", 0, P // 16), BL, "LT", PAD, PAD + P) if t == 2 else None
        st["locc"] = lambda: cp(ap("LOC", 0, P // 16), ap("PS6", 0, P // 16)) if t == 2 else None
        st.update(amended(t))

        def go_one():
            ts(ap("C0"), far(0), TH, None, ALU.is_lt)
            run("v", [ap("C0"), IN7], [ap("SC")], lambda: g.vector.tensor_tensor_scan(T.SC[:], T.C0[:], T.C0[:], IN7[3], ALU.add, ALU.max))
            tt(ap("C1"), ap("C0"), FL, ALU.mult)
            mm(ap(FB[0], 128, 256), [(W0, ap("C0")), (NBK, ap("SC")), (W1, ap("C1")), (NW0, ap("C1"))])

        def list_one(a):
            tt(ap("TM", a, a + 128), ap("SLOT", a, a + 128), ap(FB[0], 128, 256), ALU.min)
            cp(ap("SL", w0 + a, w0 + a + 128), ap("TM", a, a + 128))

        def locp(q):
            a, n = (t - 1) * P // 2, P // 32
            if q == "p":
                wrap(ap("PS6", 0, n), BL, "LT", PAD + a, PAD + a + P // 2)
            else:
                cp(ap("LOC", a // 16, a // 16 + n), ap("PS6", 0, n))

        def firsts2():
            turned(ap("PS4", 0, 128), 0)
            turned(ap("PS4", 128, 256), 256)
            act(ap("SDO"), ap("PS4", 0, 256))
            send(ap("SDI"), ap("SDO"), "asc")

        st["g1"], st["ts"], st["tc"], st["f2"] = go_one, lambda: list_one(0), lambda: list_one(128), firsts2
        st["lp"], st["lv"] = lambda: locp("p"), lambda: locp("v")
        st["ps"] = lambda: pick("PS5", 0, "DG", 0, 2, 4)
        st["pt"] = lambda: pick("PS5", 256, "MB", 0, 2, 4)
        st["ea"] = lambda: act(ap("ET"), ap("PS5"))
        st["pm"] = lambda: pick("PS3", 256, "LT", PAD + P, 2, 4)
        st["em"] = lambda: act(ap("ET", 0, 256), ap("PS3", 256, 512))
        st["lm"] = lambda: turned(ap("PS3", 0, 128), 0)
        st["dd0"] = lambda: tt(ap("SDI", 128, 256), ap("SDI", 128, 256), ap("SDI", 0, 128), ALU.subtract, ext=[("asc", nin)])
        st["u1G"] = u1_g
        st["uA"], st["nhA"], st["u1A"] = kept_a, hits_a, u1_a
        st["snA"] = lambda: mm(SWP, [(I32, ap(cur))], True, False)
        st["slotA"] = lambda: act(ap("SLOT"), SWP)
        st["watch"] = lambda: watch(t, 0.0)
        st["dd"] = lambda: tt(ap("SDI", 128, 256), ap(TL[0], TL[1], TL[1] + 128), call(cur), ALU.subtract)
        st["locm"] = lambda: wrap(ap("PS3", 0, 128), BL, "LT", PAD + P, YC)
        for name in plan(t):
            if ":" in name:
                a, b = [128 * int(x) for x in name[2:].split(":")]
                if name[0] == "w":
                    st[name] = lambda q=name[1], a=a, b=b: look(q, a, b, int(a >= EP[1]))
                else:
                    st[name] = lambda q=name[1], a=a, b=b: turn(q, a, b)
        for q in "av":
            for c in range(4):
                st["w%s%d" % (q, c)] = lambda q=q, c=c: look(q, c * CH, (c + 1) * CH, int(c * CH >= EP[1]))
                st["i%s%d" % (q, c)] = lambda q=q, c=c: turn(q, c * CH, (c + 1) * CH)
                st["y%s%d" % (q, c)] = lambda q=q, c=c: begin(q, c)
            for h in range(2):
                st["Y%s%d" % (q, h)] = lambda q=q, h=h: begin(q, h, M // 2)
                st["o%s%d" % (q, h)] = lambda q=q, h=h: first(q, "DG", h, 0)
                st["o%s%d" % (q, h + 2)] = lambda q=q, h=h: first(q, "MB", h, 128)
                st["W%s%d" % (q, h)] = lambda q=q, h=h: look(q, EH[h], EH[h + 1], int(EH[h] >= EP[1]))
                st["I%s%d" % (q, h)] = lambda q=q, h=h: turn(q, EH[h], EH[h + 1])
        return st

    def results():
        cur = S[(RO - 1) % 2]
        st = {}

        def store(a, b):
            o = span("X", OB[a], OB[b], PAD)
            stores.append(dma("s", T.yx[:, OB[a]:OB[b]], o[3], [o], []))

        def small(y, i):
            o = ap("FIN", 128 * i, 128 * i + 128)
            stores.append(dma("s", y[:], o[3], [o], []))

        def hits():
            act(ap("NHB"), NH)
            mm(PAIR, [(PMB, ap("NHB"))])

        def trigs():
            watch(RO, float(-PAD))
            tt(ap("FIN", 128, 256), ap("TR", 0, 128), ap("TR", 128, 256), ALU.add)
            small(T.ytrig, 1)

        def srcs():
            for p in range(2):
                tt(half("U0", p), shalf(cur, p), half("PS4", p), ALU.mult)
            tt(ap("PS2", 0, 128), ap("U0", 0, 128), ap("PS5", 0, 128), ALU.add)
            ts(ap("FIN", 0, 128), ap("PS2", 0, 128), float(-PAD), None, ALU.add)
            small(T.ysrc, 0)

        def swap():
            flips(RO)
            mm(ap("PS4", 256, 384), [(IB, FL)])
            tt(ap("U1", 0, 128), TG, ap("PS4", 256, 384), ALU.mult)
            mm(ap("PS3", 128, 256), [(SWI, ap("U1", 0, 128))])

        def targets():
            tt(ap("FIN", 256, 384), TG, ap("PS3", 128, 256), ALU.add)
            small(T.ytg, 2)

        OB = CFG["o"]
        for c in range(len(OB) - 1):
            a, b = OB[c], OB[c + 1]
            st["ov%d" % c] = lambda a=a, b=b: ts(span("X", a, b, PAD), ZA, om, ob, ALU.mult, ALU.add, off=lspan("LOC", a, b))
            st["oa%d" % c] = lambda a=a, b=b: act(span("X", a, b, PAD), ZA, bias=ob, scale=om, off=lspan("LOC", a, b))
            for e in range(c + 1, len(OB)):
                st["st%d_%d" % (c, e)] = lambda c=c, e=e: store(c, e)
        for p in range(2):
            st["nh%d" % p] = lambda p=p: wrap(half("PS4", p), BH, "I2", EH[p], EH[p + 1])
            st["n%d" % p] = lambda p=p: wrap(half("PS5", p), BS, "I2", EH[p], EH[p + 1])
        st.update(amended(RO))
        st["nhb"], st["trigs"], st["srcs"], st["swap"], st["targets"] = hits, trigs, srcs, swap, targets
        st["xp"] = lambda: act(ap("XP"), PAIR, ACT.Abs, bias=-1.0)
        return st

    for t in range(RO):
        st, nxt = steps(t), steps(t + 1) if t < RO - 1 else results()
        for name in plan(t):
            if name.endswith("+"):
                nxt[name[:-1]]()
            else:
                st[name]()

    for tok in stores:
        wait("s", tok)
    g.wait_ge(T.sem.sent, sent[0])
    for s in ("qv", "qa", "qp", "qg"):
        wait("g", (s, count[s]))
